import numpy as np, ml_dtypes
CORES = [40,41,42,43,44,45,46,47]
N = 8
BF = ml_dtypes.bfloat16
V, X, PS, RO, EP = 2048, 256, 64, 2, 3
K = V // PS; W = V + (N - 1) * X
def blocks(a):
    return np.repeat(np.swapaxes(a, -1, -2), PS, axis=-1)
def kin(rng):
    sh = (N, 8, 16, V); u = rng.random(sh)
    a = blocks(rng.integers(0, K, (8, K, 16))) * PS + rng.integers(0, PS, sh)
    return np.where(u > 0.95, np.arange(V), np.where(u < 0.5, a, rng.integers(0, W, sh)))
def parts(rng):
    sh = (N, 8, 16, V)
    p = rng.choice(np.array([0.3, 0.6, 0.8, 0.95]), (8, K, 16))
    s = np.maximum(rng.integers(40, 256, (8, K, 16)) * rng.choice(np.array([0.25, 0.5, 1.0]), (N, 8, K, 16)), 1.0)
    w = np.where(rng.random(sh) < blocks(p), 1 + (rng.random(sh) * blocks(s)).astype(np.int64), 0)
    l = kin(rng); r = kin(rng)
    same = rng.random((8, K)) < 0.25; same[np.arange(8), rng.integers(0, K, 8)] = True
    r = np.where(np.repeat(same, PS, axis=1)[:, None, :], l, r)
    return w, l, r
def pack(w, l, r):
    return {"w": np.ascontiguousarray(w).reshape(N, 128, V).astype(np.float32).astype(BF), "kids": np.ascontiguousarray(l + 4096 * r).reshape(N, 128, V).astype(np.int32)}
def setup_inputs(rng):
    w, l, r = parts(rng)
    return pack(w, l, r)
KL = np.array([1, 2, 6, 4, 5, 6, 6, 7, 6, 9, 11, 11, 13, 14, 12, 11])
KR = np.array([1, 2, 6, 4, 5, 7, 6, 7, 8, 9, 12, 11, 13, 14, 12, 6])
HQ = np.array([100, 100, 100, 100, 100, 100, 100, 60, 60, 0, 120, 20, 100, 100, 100, 120])
def crypt(rng, w, l, r, g):
    ops = [int(i) for i in 1 + rng.permutation(15)[:5]]; q, p, u = ops[:3]
    z = 2 * PS; h = PS // 4; cp = h // 8; s = z + 2 * h; e = z + PS
    w[:, g, :, z:e] = 0; w[:, g, p, z:z + h] = 255
    nul = z + h + rng.integers(0, h, (N, 1, h)); l[:, g, :, z:z + h] = nul; r[:, g, :, z:z + h] = nul
    at = s + np.arange(16)[:, None] * cp + np.arange(cp)
    l[:, g, :, s:e] = at[KL].reshape(-1); r[:, g, :, s:e] = at[KR].reshape(-1)
    w[:, g, q, s:e] = np.repeat(HQ, cp)
    w[:, g, 0, s + 9 * cp:s + 10 * cp] = 100; w[:, g, u, s + 6 * cp:s + 7 * cp] = 50
    return at, ops
def seat(rng, w, l, r, g, k, ops, x, y):
    e = slice(k * PS, k * PS + PS); q, u = ops[0], ops[2]
    w[:, g, :, e] = rng.integers(0, 51, (N, 16, PS)); w[:, g, 0, e] = 0; w[:, g, u, e] = 0
    w[:, g, q, e] = rng.integers(200, 256, (N, PS)); l[:, g, q, e] = x; r[:, g, q, e] = y
def lone(rng, w, l, r, g, n):
    at, ops = crypt(rng, w, l, r, g); cp = at.shape[1]; bl = [k for k in range(K) if k != 2]
    for j in range(N + 1):
        m = rng.random((N, PS)) < 0.5
        if j < N:
            m = np.zeros((N, PS), bool); m[j, rng.integers(0, PS)] = True
        x = at[3 - n + 3 * m, rng.integers(0, cp, (N, PS))]
        seat(rng, w, l, r, g, bl[j], ops, x, x)
def stage(rng, w, l, r, g):
    at, ops = crypt(rng, w, l, r, g); cp = at.shape[1]; q, p, u, a, b = ops; sh = (N, PS)
    def some(j):
        return at[j, rng.integers(0, cp, sh)]
    y = some(6); w[:, g, :, :PS] = 0; w[:, g, u, :PS] = rng.integers(200, 256, sh); l[:, g, u, :PS] = y; r[:, g, u, :PS] = y
    x = some(8); seat(rng, w, l, r, g, 1, ops, x, x)
    x = some(9); seat(rng, w, l, r, g, 3, ops, x, x)
    m = np.argsort(rng.random(sh), axis=1) < 5 * PS // 8; i = rng.integers(0, cp, sh)
    seat(rng, w, l, r, g, 4, ops, at[np.where(m, 14, 10), i], at[np.where(m, 11, 12), i])
    seat(rng, w, l, r, g, 5, ops, some(15), some(12))
    x = V + rng.integers(0, N - 1, sh) * X + rng.integers(0, PS, sh); seat(rng, w, l, r, g, 6, ops, x, x)
    x = some(6); seat(rng, w, l, r, g, 7, ops, x, x + V)
    x = some(6); seat(rng, w, l, r, g, 8, ops, x, x + 2048)
    e = slice(9 * PS, 10 * PS); lo, hi = min(a, b), max(a, b); x = some(6); y = some(7)
    seat(rng, w, l, r, g, 9, ops, x, x); w[:, g, q, e] = rng.integers(100, 150, sh)
    v = rng.integers(150, 255, N * PS); v[0] ^= np.add.reduce(v) & 1
    o = rng.permutation(v); o[np.argmin(o)] += 1
    w[:, g, lo, e] = v.reshape(sh); w[:, g, hi, e] = o.reshape(sh)
    l[:, g, lo, e] = x; r[:, g, lo, e] = x; l[:, g, hi, e] = y; r[:, g, hi, e] = y
def setup_inputs_twin(rng):
    w, l, r = parts(rng); P = PS
    w[:, :2, :, :P] = 255
    w[:, :2, :, P:2 * P] = rng.integers(200, 256, (N, 2, 16, P))
    w[:, :2, :, 2 * P:3 * P] = rng.integers(100, 151, (N, 2, 16, P))
    w[:, :2, :, 3 * P:4 * P] = np.where(rng.random((N, 2, 16, P)) < 0.6, rng.integers(1, 10, (N, 2, 16, P)), 0)
    c = 2 * P + rng.integers(0, P, (N, 2, 1, P))
    l[:, :2, :, :P] = c; r[:, :2, :, :P] = P + np.arange(P)
    l[:, :2, :, P:2 * P] = 3 * P + rng.integers(0, P, (N, 2, 16, P)); r[:, :2, :, P:2 * P] = c
    l[:, :2, :, 2 * P:3 * P] = 3 * P + rng.integers(0, P, (N, 2, 16, P)); r[:, :2, :, 2 * P:3 * P] = 3 * P + rng.integers(0, P, (N, 2, 16, P))
    odd = np.arange(1, K, 2) * P + P - 1
    big = w[N - 1, 4:6]; big[:, :, odd] = 255
    r[:, 4:7] = np.where(w[:, 4:7] == 0, rng.integers(0, W, (N, 3, 16, V)), l[:, 4:7])
    sub = r[N - 1, 4:6]; sub[:, :, odd] = (l[N - 1, 4:6][:, :, odd] + 1) % W
    lone(rng, w, l, r, 2, 1); stage(rng, w, l, r, 3); lone(rng, w, l, r, 7, RO - 1)
    return pack(w, l, r)
def setup_inputs_ties(rng):
    w, l, r = parts(rng); h = (K // 2) * PS
    w[:, 0] = 255
    w[:, 1] = np.where(w[:, 1] > 0, 9, 0)
    for g in (1, 4, 5): w[:, g, 1::2] = w[:, g, 0::2]
    w[:, 6] = np.minimum(w[:, 6], 2)
    w[:, 2:4, :, :h] = 255
    a = h + rng.integers(0, V - h, (N, 2, 16, h)); l[:, 2:4, :, :h] = a
    r[:, 2:4, :, :h] = a.reshape(N, 2, 16, K // 2, PS)[..., rng.permutation(PS)].reshape(N, 2, 16, h)
    e = (K - 2) * PS; f = (K - 1) * PS
    w[:, 7, :, :2 * PS] = 255; w[:, 7, :, e:] = 0
    w[:, 7, 9, e:f] = 100; w[:, 7, 2, f:] = 100
    l[:, 7, :, :2 * PS] = e + rng.integers(0, PS, (N, 16, 2 * PS)); r[:, 7, :, :2 * PS] = f + rng.integers(0, PS, (N, 16, 2 * PS))
    l[:, 7, :, e:f] = f + rng.integers(0, PS, (N, 16, PS)); r[:, 7, :, e:f] = f + rng.integers(0, PS, (N, 16, PS))
    l[:, 7, :, f:] = e + rng.integers(0, PS, (N, 16, PS)); r[:, 7, :, f:] = e + rng.integers(0, PS, (N, 16, PS))
    return pack(w, l, r)
def setup_inputs_scarce(rng):
    w, l, r = parts(rng); q = rng.permutation(N)
    w = np.where(rng.random(w.shape) < blocks(rng.choice(np.array([0.1, 0.3, 0.6]), (8, K, 16))), w, 0)
    w[q[0], 4:] = 0; w[:, 0, :, :PS] = 0
    w[:, 1, :, 2 * PS:3 * PS] = 0; v = 2 * PS + 5
    w[q[1], 1, :, v] = 255; l[q[1], 1, :, v] = V; r[q[1], 1, :, v] = W - 1
    w[:, 1, :, 0] = 200; w[:, 1, :, X - 1] = 100
    return pack(w, l, r)
def setup_inputs_ends(rng):
    w, l, r = parts(rng); e = np.array([0, V - 1, V, W - 1, X - 1])
    for g in (0, 3, 6):
        l[:, g] = rng.choice(e, (N, 16, V)); r[:, g] = rng.choice(e, (N, 16, V))
    for g in (1, 5): l[:, g] = np.where(rng.random((N, 1, V)) < 0.4, np.arange(V), l[:, g])
    l[:, 2] = rng.integers(V, W, (N, 16, V)); r[:, 2] = rng.integers(V, W, (N, 16, V)); w[:, 2] = np.maximum(w[:, 2], 1)
    l[:, 4] = rng.integers(0, V, (N, 16, V)); r[:, 4] = rng.integers(0, V, (N, 16, V))
    r[:, 7] = np.where(rng.random((N, 16, V)) < 0.5, np.arange(V), r[:, 7])
    return pack(w, l, r)
def setup_inputs_spread(rng):
    w, l, r = parts(rng); sh = w.shape
    w = np.minimum((np.exp2(8 * rng.random((N, 8, 1, V))) * rng.random(sh)).astype(np.int64), 255)
    l = np.where(rng.random(sh) < 0.5, np.minimum((W * rng.random(sh) ** 3).astype(np.int64), W - 1), l)
    return pack(w, l, r)
def check_inputs(d):
    bad = []; v = d["w"].astype(np.float32); k = d["kids"].astype(np.int64)
    if not np.all((v >= 0) & (v <= 255) & (v == np.floor(v))): bad.append("whole numbers of w")
    if np.min(k) < 0 or np.max(k & 4095) >= W or np.max(k >> 12) >= W: bad.append("class numbers of kids")
    return bad
def pick(tab, o, c):
    return np.take_along_axis(tab.reshape(N, 8, 16 * W), o * W + c, 2)
def reference(w, kids):
    tw = w.astype(np.float32).astype(np.int64).reshape(N, 8, 16, V); kd = kids.astype(np.int64).reshape(N, 8, 16, V)
    tl = kd & 4095; tr = kd >> 12; own = np.arange(V)
    ghost = np.broadcast_to(np.arange(V, W), (N, 8, 16, W - V))
    for ep in range(EP):
        fw = np.stack([np.concatenate([tw[a]] + [tw[(a - d) % N][:, :, :X] for d in range(1, N)], axis=2) for a in range(N)])
        fl = np.concatenate([tl, ghost], axis=3); fr = np.concatenate([tr, ghost], axis=3)
        live = np.ones((N, 8, V), bool); b = np.zeros((RO + 1, N, 8, V), np.int64); b[0] = own
        have = np.zeros((RO + 1, 8, K), bool); have[0] = True; x = []
        for t in range(1, RO + 1):
            U = np.zeros((8, K, t, 16), np.int64)
            for h in range(t):
                m = np.minimum(np.take_along_axis(fw, b[h][:, :, None, :], 3), tw) * live[:, :, None, :]
                s = np.add.reduce(np.add.reduce(m.reshape(N, 8, 16, K, PS), axis=4), axis=0)
                U[:, :, h] = np.where(have[h][:, :, None], s.transpose(0, 2, 1), -1)
            best = np.argmax(U.reshape(8, K, t * 16), axis=2)
            bh = np.repeat(best >> 4, PS, axis=1); bo = np.repeat(best & 15, PS, axis=1)
            cur = np.take_along_axis(b, np.broadcast_to(bh, (1, N, 8, V)), 0)[0]; x.append(cur)
            live = live & (pick(fw, bo, cur) > 0)
            lk = pick(fl, bo, cur); rk = pick(fr, bo, cur)
            b = np.where(np.arange(RO + 1)[:, None, None, None] == bh, lk, b); b[t] = rk
            drop = np.zeros((8, K), bool)
            for h in range(t):
                differ = np.any((live & (rk != b[h])).reshape(N, 8, K, PS), axis=(0, 3))
                drop = drop | (have[h] & ~differ)
            have[t] = ~drop
        lf = np.concatenate([live, np.zeros((N, 8, W - V), bool)], axis=2); die = np.zeros((N, 8, V), bool)
        for c in x[1:]: die = die | (np.take_along_axis(lf, c, 2) & (c != own))
        go = (live & ~die)[:, :, None, :]
        h0 = b[0]; h1 = b[0]
        for t in range(RO, 0, -1): h1 = np.where(np.repeat(have[t], PS, axis=1), b[t], h1)
        h0 = h0[:, :, None, :]; h1 = h1[:, :, None, :]
        nw = (np.take_along_axis(fw, h0, 3) + np.take_along_axis(fw, h1, 3)) >> 1
        tw = np.where(go, nw, tw); tl = np.where(go, h0, tl); tr = np.where(go, h1, tr)
    return {"yw": tw.reshape(N, 128, V).astype(np.float32).astype(BF), "yk": (tl + 4096 * tr).reshape(N, 128, V).astype(np.float32)}

@@ -1,0 +1,732 @@
+import math
+import numpy as np
+from concourse.bass import DstId, RemoteDMATransfer
+from concourse.mybir import AluOpType, AxisListType, ActivationFunctionType
+
+ALU = AluOpType
+ACTF = ActivationFunctionType
+N, V, X, EP = 8, 2048, 256, 3
+PAD = 16
+WIN = PAD + V + (N - 1) * X
+OFF = PAD * 4097
+TWO24 = float(2 ** 24)
+MAGIC = 1.5 * 2 ** 23
+EPS = 2.0 ** -11
+
+SCRATCH = {}
+SIZE = {"float32": 4, "int32": 4, "bfloat16": 2, "float16": 2, "uint16": 2}
+
+
+def _decl(names, cols, dtype, where="sbuf"):
+    for n in names.split():
+        SCRATCH[n] = (where, [128, cols], dtype)
+
+
+_decl("W0 W1 NL", WIN, "bfloat16")
+_decl("TK", WIN, "float32")
+_decl("KG KR", V, "int32")
+_decl("WE M0 M1 RL DG WO repb ext", V, "bfloat16")
+_decl("KX GA YY YK repf", V, "float32")
+_decl("S16", V, "float16")
+_decl("coli ci", 256, "int32")
+_decl("pi", 16, "int32")
+_decl("pf", 24, "float32")
+_decl("rowm sc0 sc1", 16, "float32")
+_decl("pbig RB0 RB1 RB2 RB3", 256, "bfloat16")
+_decl("idh", 128, "float16")
+_decl("oselh", 32, "float16")
+_decl("oselb oseln", 32, "bfloat16")
+_decl("idf blk sel32 RF0 RF1 RF2 RF3 AA AT LA kvm vid EE0 EE1 FF0 FF1 LL0 LL1", 128, "float32")
+_decl("seln selj oh0 oh1 ohT0 ohT1 junk0 junk1", 64, "float32")
+_decl("tb tm", 80, "bfloat16")
+_decl("XS0 XS1 XS2 XS3", 80, "float32")
+_decl("bb0 bb1 lr0 lr1 ti0 ti1", 128, "int32")
+_decl("wk0 wk1", 1536, "float32")
+_decl("lv l1 idn", 128, "bfloat16")
+_decl("selnb seljb", 64, "bfloat16")
+_decl("vidu bu0 bu1 lu0 lu1 xu du", 128, "uint16")
+_decl("soff", 4, "uint16")
+_decl("PA0 PA1 PG0 PG1 PG2 PG3 PG4 PV", 512, "float32", "psum")
+for _h in range(2):
+    SCRATCH["kt%d" % _h] = ("sbuf", [128, 8, 2, 8], "float32")
+    SCRATCH["lt%d" % _h] = ("sbuf", [128, 8, 2, 8], "bfloat16")
+    for _n, _d in (("dW", "bfloat16"), ("rW", "bfloat16"), ("dK", "int32"), ("rK", "int32"), ("eW", "bfloat16"), ("sW", "bfloat16")):
+        SCRATCH["%s%d" % (_n, _h)] = ("dram", [N, 128, 128], _d)
+
+NDMA = 32
+SEMAPHORES = ["cP", "cD", "cA", "cG", "sent"] + ["dm%d" % k for k in range(NDMA)] + ["ar%d" % k for k in range(7)]
+ALL = slice(None)
+
+
+def vw(name, a=0, b=None, s=1, p=None):
+    if b is None:
+        b = SCRATCH[name][1][-1]
+    return ("v", name, a, b, s, p)
+
+
+def ind(name, offs, a=0, b=None):
+    return ("i", name, offs, a, SCRATCH[name][1][-1] if b is None else b)
+
+
+def raw(name, index, n=0, part=(0, 1 << 30)):
+    return ("r", name, index, n, part)
+
+
+def ap(T, v):
+    if not isinstance(v, tuple):
+        return v
+    if v[0] == "v":
+        rows = ALL if v[5] is None else slice(v[5][0], v[5][1])
+        cols = slice(v[2], v[3]) if v[4] == 1 else slice(v[2], v[3], v[4])
+        return T[v[1]][rows, cols]
+    if v[0] == "i":
+        return T[v[1]][:, v[3]:v[4]].indirect(ap(T, v[2]))
+    return T[v[1]][v[2]]
+
+
+def regions(v):
+    if not isinstance(v, tuple):
+        return []
+    if v[0] == "v":
+        if SCRATCH[v[1]][0] == "psum":
+            return [(v[1], 0, 512)]
+        return [(v[1], v[2], v[3])]
+    if v[0] == "i":
+        return [(v[1], v[3], v[4])] + regions(v[2])
+    return [(v[1],) + v[4]]
+
+
+def count(v):
+    if v[0] == "r":
+        return v[3]
+    if v[0] == "i":
+        return 16 * count(v[2])
+    return len(range(v[2], v[3], v[4]))
+
+
+def width(v):
+    return SIZE[SCRATCH[v[1]][2]]
+
+
+def in_psum(v):
+    return SCRATCH[v[1]][0] == "psum"
+
+
+CY, PCY, HOP = 1.04, 0.6, 100.0
+ON_SCALAR = {(0, 1, 0), (0, 1, 1), (1, 1, 1)}
+
+
+def build(rank, T, topo):
+    ops = []
+
+    def add(alts, outs, ins, kind="c", lat=0.0, after=()):
+        rd, wr = [], []
+        for v in ins:
+            rd += regions(v)
+        for v in outs:
+            if v[0] == "i":
+                wr += regions(v)[:1]
+                rd += regions(v)[1:]
+            else:
+                wr += regions(v)
+        ops.append({"alts": alts, "rd": rd, "wr": wr, "kind": kind, "lat": lat, "after": list(after)})
+        return len(ops) - 1
+
+    def vcost(out, ins, two=False):
+        n = count(out)
+        if out[0] == "i":
+            return 60 + n * 3.8 * CY
+        if ins[0][0] == "i":
+            return 60 + n * 1.56 * CY
+        f = 1.0
+        if two:
+            f = 1.0 if (in_psum(ins[0]) or in_psum(ins[1])) else 2.0
+        elif width(out) == 2 and width(ins[0]) == 2:
+            f = 0.5
+        return 30 + max(64, n * f) * CY
+
+    def ts_alt(out, a, s1, op0, s2=None, op1=None):
+        def emit(g):
+            if op1 is None:
+                return g.vector.tensor_scalar(ap(T, out), ap(T, a), ap(T, s1), None, op0)
+            return g.vector.tensor_scalar(ap(T, out), ap(T, a), ap(T, s1), ap(T, s2), op0, op1)
+        return (emit, vcost(out, [a]))
+
+    def act_alt(out, a, func, scale, bias, acc):
+        def emit(g):
+            if acc is None:
+                return g.scalar.activation(ap(T, out), ap(T, a), func, bias=ap(T, bias), scale=ap(T, scale))
+            return g.scalar.activation(ap(T, out), ap(T, a), func, bias=ap(T, bias), scale=ap(T, scale), accum_out=ap(T, acc))
+        return (emit, 70 + count(out) * (1.56 if a[0] == "i" else 1.0) * CY)
+
+    def ts(out, a, s1, op0, s2=None, op1=None):
+        return add({"D": ts_alt(out, a, s1, op0, s2, op1)}, [out], [a, s1, s2])
+
+    def act(out, a, func, scale=1.0, bias=0.0, acc=None):
+        return add({"A": act_alt(out, a, func, scale, bias, acc)}, [out] + ([acc] if acc else []), [a, scale, bias])
+
+    def aff(out, a, scale=1.0, bias=0.0):
+        return add({"A": act_alt(out, a, ACTF.Identity, scale, bias, None), "D": ts_alt(out, a, scale, ALU.mult, bias, ALU.add)}, [out], [a, scale, bias])
+
+    def above(out, a, scale=1.0):
+        return add({"A": act_alt(out, a, ACTF.Sign, scale, 0.0, None), "D": ts_alt(out, a, scale, ALU.mult, 0.0, ALU.is_gt)}, [out], [a, scale])
+
+    def tt(out, a, b, op):
+        return add({"D": (lambda g: g.vector.tensor_tensor(ap(T, out), ap(T, a), ap(T, b), op), vcost(out, [a, b], True))}, [out], [a, b])
+
+    def cp(out, a):
+        return add({"D": (lambda g: g.vector.tensor_copy(ap(T, out), ap(T, a)), vcost(out, [a]))}, [out], [a])
+
+    def red(out, a):
+        return add({"D": (lambda g: g.vector.tensor_reduce(ap(T, out), ap(T, a), AxisListType.X, ALU.max), 30 + max(64, count(a)) * CY)}, [out], [a])
+
+    def tr(out, a):
+        return add({"D": (lambda g: g.vector.transpose(ap(T, out), ap(T, a)), vcost(out, [a]))}, [out], [a])
+
+    def ms(out, c):
+        return add({"D": (lambda g: g.vector.memset(ap(T, out), c), 30 + max(64, count(out) * width(out) / 4) * CY)}, [out], [])
+
+    def mm(items):
+        def emit(g):
+            r = None
+            for (o, l, x, st, sp) in items:
+                r = g.tensor.matmul(ap(T, o), ap(T, l), ap(T, x), st, sp)
+            return r
+        c = 40 + sum(max(min(64, count(l)), count(x)) * (4 if width(x) == 4 else 1) * PCY for (o, l, x, st, sp) in items)
+        return add({"P": (emit, c)}, [i[0] for i in items], [i[1] for i in items] + [i[2] for i in items])
+
+    def iota(out, pattern, base, mult):
+        return add({"G": (lambda g: g.iota(ap(T, out), pattern, base, mult), 130 + 2 * count(out) * CY)}, [out], [])
+
+    def dma(q, out, src, nbytes, after=(), also=None):
+        def emit(g):
+            e = g.sync if q == "S" else g.scalar
+            return e.dma_start(ap(T, out), ap(T, src))
+        return add({q: (emit, 60)}, [out], [src, also], "d", 2000 + nbytes / 200.0, after)
+
+    me = T.cores[rank]
+    peers = [(rank + d) % N for d in range(1, N)]
+    far = [r for r in peers if topo.die(T.cores[r]) != topo.die(me)]
+    near = [r for r in peers if topo.die(T.cores[r]) == topo.die(me)]
+    masks = {}
+    for lst, first in ((far, 0), (near, 1)):
+        for k, r in enumerate(lst):
+            e = topo.engines(me, T.cores[r])[first::2]
+            masks[r] = (1 << e[2 * k]) | (1 << e[2 * k + 1])
+    nsend = [0]
+
+    def exchange(src_of, dst, land, nbytes):
+        k = nsend[0]
+        nsend[0] += 1
+
+        def emit(g):
+            trs = []
+            for r in peers:
+                rid, pid, se = topo.addr(T.cores[r])
+                trs.append(RemoteDMATransfer(dst_ids=[DstId(rid=rid, pnc=pid)], dma_engine_mask=masks[r], remote_sem=T.sem["ar%d" % k],
+                                             src=ap(T, src_of(r)), dst=ap(T, dst)))
+            return g.remote_dma_fused(trs, local_sem=T.sem.sent)
+        s = add({"G": (emit, 300)}, [], [src_of(r) for r in peers], "s")
+        i = add({"X": (None, 0)}, land, [], "a", 2200 + nbytes / 30.0, [s])
+        ops[i]["sem"] = ("ar%d" % k, 2 * (N - 1))
+        return i
+
+    rows = slice(16 * rank, 16 * rank + 16)
+    first = {}
+    for h in range(2):
+        cs = slice(1024 * h, 1024 * h + 1024)
+        for src, k, to, at, nb in (("w", "W", "W0", PAD, 262144), ("kids", "K", "KG", 0, 524288)):
+            d, r = "d%s%d" % (k, h), "r%s%d" % (k, h)
+            q = "A" if (k, h) == ("K", 0) else "S"
+            first[k] = dma(q, raw(d, ALL), raw(src, (ALL, cs)), nb, [first[k]] if h else [])
+            dma(q, raw(r, rank), raw(src, (rows, cs)), nb // N, [first[k]] if h else [])
+            exchange(lambda x, d=d: raw(d, x), raw(r, rank), [raw(r + "in", 0)], nb // N)
+            ld = dma("S", vw(to, at + 1024 * h, at + 1024 * h + 1024), raw(r, ALL), nb, also=raw(r + "in", 0))
+    dma("S", vw("KR"), raw("kids", ALL), 1048576, [ld])
+
+    def P(k):
+        return vw("pf", k, k + 1)
+
+    def vid(h):
+        return vw("PV", 64 * h, 64 * h + 64)
+
+    iota(vw("coli"), [[1, 256]], 0, 0)
+    iota(vw("pi", 0, 1), [[1, 1]], 0, 1)
+    AND, SHR = ALU.bitwise_and, ALU.arith_shift_right
+    spec = [None, (15, None), (None, 4), (1, 4), (63, None), (None, 6), (1, None), (None, 1), (7, None), (1, 3), (None, 5)]
+    for k, sp in enumerate(spec):
+        if sp is None:
+            continue
+        o, a = vw("pi", k, k + 1), vw("pi", 0, 1)
+        if sp[1] is None:
+            ts(o, a, sp[0], AND)
+        elif sp[0] is None:
+            ts(o, a, sp[1], SHR)
+        else:
+            ts(o, a, sp[1], SHR, sp[0], AND)
+    cp(vw("pf", 0, 11), vw("pi", 0, 11))
+    aff(P(11), P(8), 128.0, float(PAD))
+    aff(P(12), P(9), 64.0, P(11))
+    aff(P(14), P(9), 64.0, P(8))
+    aff(P(13), P(10), 16.0, P(14))
+    for k in range(2):
+        ts(P(15 + k), P(5), float(k), ALU.is_equal)
+        ts(P(17 + k), P(6), float(k), ALU.is_equal)
+    for h in range(2):
+        ts(vw("vid", 64 * h, 64 * h + 64), vw("coli", 0, 64), P(12), ALU.add, 1024.0 * h, ALU.add)
+    ts(vw("vidu", 0, 64), vw("vid", 0, 64), -float(PAD), ALU.add)
+    for b in ("W0", "W1", "TK", "NL"):
+        ms(vw(b, 0, PAD), 0.0)
+    ms(vw("NL", PAD + V, WIN), 1.0)
+    for k in range(4):
+        ms(vw("RB%d" % k), 0.0)
+        ms(vw("RF%d" % k), 0.0)
+    ts(vw("ci", 0, 128), vw("coli", 0, 128), 15, AND)
+    ts(vw("oselb"), vw("ci", 0, 32), P(1), ALU.is_equal)
+    ts(vw("oselh"), vw("ci", 0, 32), P(1), ALU.is_equal)
+    aff(vw("oseln"), vw("oselb"), -1.0)
+    ts(vw("sel32"), vw("ci", 0, 128), P(1), ALU.is_equal, 32.0, ALU.mult)
+    ts(vw("idf"), vw("coli", 0, 128), P(0), ALU.is_equal)
+    cp(vw("idh"), vw("idf"))
+    aff(vw("pbig", 0, 128), vw("idf"))
+    aff(vw("pbig", 128, 256), vw("idf"))
+    aff(vw("idn"), vw("idf"), -1.0)
+    ts(vw("ci", 128, 192), vw("coli", 0, 64), 4, SHR, 1, AND)
+    ts(vw("tm", 0, 64), vw("ci", 128, 192), P(3), ALU.not_equal, -float(2 ** 23), ALU.mult)
+    ts(vw("tb", 0, 32), vw("ci", 0, 32), -1.0, ALU.mult, 31.0, ALU.add)
+    ts(vw("tb", 32, 64), vw("ci", 0, 32), -1.0, ALU.mult, 15.0, ALU.add)
+    ms(vw("tb", 64, 80), 0.0)
+    ms(vw("tm", 64, 80), 0.0)
+    for cc in range(4):
+        ts(vw("soff", cc, cc + 1), P(13), float(128 * (cc // 2) + 8 * (cc % 2)), ALU.add)
+    ts(vw("seln"), vw("coli", 0, 64), P(4), ALU.is_equal)
+    ts(vw("selj"), vw("coli", 0, 64), P(7), ALU.is_equal)
+    aff(vw("selnb"), vw("seln"))
+    aff(vw("seljb"), vw("selj"))
+    ts(vw("ti1"), vw("coli", 0, 128), 4, SHR)
+    ts(vw("blk"), vw("ti1"), P(2), ALU.is_equal)
+    ts(vw("rowm"), vw("coli", 0, 16), P(1), ALU.is_equal)
+    for i in range(16):
+        aff(vw("repf", 128 * i, 128 * i + 128), vw("blk"), vw("rowm", i, i + 1))
+        aff(vw("repb", 128 * i, 128 * i + 128), vw("blk"), vw("rowm", i, i + 1))
+        aff(vw("ext", 128 * i, 128 * i + 128), vw("pbig", 0, 128), vw("rowm", i, i + 1))
+    for j in range(N - 1):
+        a = PAD + V + X * j
+        ts(vw("TK", a, a + X), vw("coli"), float(a), ALU.add, 4097.0, ALU.mult)
+    mm([(vw("PV", 0, 128), vw("idf"), vw("vid"), True, True)])
+
+    big = [0]
+
+    def bank():
+        big[0] += 1
+        return "PG%d" % (big[0] % 5)
+
+    def part_of(kk):
+        return kk // 2 + 8 * (kk % 2)
+
+    def wk(h, k):
+        return vw("wk%d" % h, 64 * k, 64 * k + 64)
+
+    def sc(h, k):
+        return vw("sc%d" % h, k, k + 1)
+
+    def spread(src, mats, q):
+        b = bank()
+        items = [(vw(b, 64 * u, 64 * u + 64), vw(mats, 128 * part_of(8 * q + u), 128 * part_of(8 * q + u) + 128), src, True, True) for u in range(8)]
+        mm(items[:4])
+        mm(items[4:])
+        return vw(b)
+
+    def sums(terms, h, hole, q):
+        o = vw("PA%d" % h, 32 * hole, 32 * hole + 32)
+        items = []
+        for b in range(4 * q, 4 * q + 4):
+            for k, (data, osel) in enumerate(terms):
+                a = 1024 * h + 128 * b
+                items.append((o, vw(data, a, a + 128), vw(osel), b == 0 and k == 0, b == 7 and k == len(terms) - 1))
+        mm(items)
+
+    def vote(t, h, exact):
+        n = 32 * t
+        n1 = n + (t - 1)
+        xs = "XS%d" % (2 * (t - 1) + h)
+        rb, rf = "RB%d" % (2 * (t - 1) + h), "RF%d" % (2 * (t - 1) + h)
+        pa = "PA%d" % h
+        if exact:
+            aff(vw(xs, 0, n), vw(pa, 0, n), 0.5, -64.0 * 1536)
+        else:
+            ts(vw(xs, 0, n), vw(pa, 0, n), MAGIC, ALU.add, MAGIC, ALU.subtract)
+        mm([(vw(pa, 0, n1), vw("pbig", 0, 128), vw("tb", 0, n1), True, False), (vw(pa, 0, n1), vw("pbig", 0, 128), vw("tm", 0, n1), False, False),
+            (vw(pa, 0, n1), vw("sel32"), vw(xs, 0, n1), False, True)])
+        red(sc(h, 0), vw(pa, 0, n))
+        ts(vw("oh%d" % h, 0, n), vw(pa, 0, n), sc(h, 0), ALU.is_equal)
+        if t == 2:
+            red(sc(h, 1), vw("oh%d" % h, 32, 64))
+            above(sc(h, 2), vw(pa, 64, 65))
+            aff(sc(h, 3), sc(h, 2), -1.0, 1.0)
+        tr(vw("ohT%d" % h, 0, n), vw("oh%d" % h, 0, n))
+        cp(ind(rb, vw("soff", 0, 2 * t)), vw("ohT%d" % h, 0, n))
+        if t == 1:
+            cp(ind(rf, vw("soff", 0, 2)), vw("ohT%d" % h, 0, 32))
+        else:
+            tt(ind(rf, vw("soff", 0, 2)), vw("ohT%d" % h, 0, 32), vw("ohT%d" % h, 32, 64), ALU.add)
+
+    def select(e, t, h, wn):
+        rb, rf = "RB%d" % (2 * (t - 1) + h), "RF%d" % (2 * (t - 1) + h)
+        pa, kt, lt, lb = "PA%d" % h, "kt%d" % h, "lt%d" % h, bank()
+        wi, ki = [], []
+        for i0 in range(8):
+            ow, ok = vw(lb, i0, 128, 8), vw(pa, i0, 128, 8)
+            if t == 1:
+                a = PAD + 1024 * h + 128 * i0
+                wi.append((ow, vw(wn, a, a + 128), vw(rb, i0, 128, 8), True, True))
+                ki.append((ok, vw("TK", a, a + 128), vw(rf, i0, 128, 8), True, True))
+            else:
+                a, b = 1024 * h + i0, 1024 * h + 1024
+                wi.append((ow, vw("M0", a, b, 8), vw(rb, i0, 128, 8), True, False))
+                wi.append((ow, vw("M1", a, b, 8), vw(rb, 128 + i0, 256, 8), False, True))
+                ki.append((ok, vw("KX", a, b, 8), vw(rf, i0, 128, 8), True, True))
+        lvh = vw("l1" if t == 1 else "lv", 64 * h, 64 * h + 64)
+        mm(wi)
+        mm(ki)
+        for k in range(2):
+            above(raw(lt, (ALL, ALL, k, ALL), 64, (k, k + 1)), vw(lb, 64 * k, 64 * k + 64), P(13 + 2 * t + k))
+        mm([(vw(lb, 128, 192), raw(lt, (ALL, ALL, ALL, ALL), 128), vw("selnb" if t == 1 else "seljb"), True, True)])
+        aff(lvh, vw(lb, 128, 192))
+        for k in range(2):
+            aff(raw(kt, (ALL, ALL, k, ALL), 64, (k, k + 1)), vw(pa, 64 * k, 64 * k + 64), P(13 + 2 * t + k))
+        kp = vw(pa, 256, 320)
+        mm([(kp, raw(kt, (ALL, ALL, ALL, ALL), 128), vw("seln" if t == 1 else "selj"), True, True)])
+        ti = vw("ti%d" % h, 64 * (t - 1), 64 * t)
+        if e == 2:
+            ts(wk(h, 0), kp, TWO24, ALU.is_lt, 1.0 / TWO24, ALU.max)
+            tt(wk(h, 16), wk(h, 0), lvh, ALU.mult)
+            tt(ti, kp, wk(h, 16), ALU.mult)
+        else:
+            tt(ti, kp, lvh, ALU.mult)
+        dst = ("bb%d" if t == 1 else "lr%d") % h
+        ts(vw(dst, 0, 64), ti, 4095, AND)
+        ts(vw(dst, 64, 128), ti, 12, SHR, 4095, AND)
+
+    def ghosts(wn):
+        for q in range(4):
+            b = bank()
+            ds = [d for d in (2 * q + 1, 2 * q + 2) if d < N]
+            mm([(vw(b, X * k, X * k + X), vw("pbig", 128 - 16 * d, 256 - 16 * d), vw(wn, PAD, PAD + X), True, True) for k, d in enumerate(ds)])
+            a = PAD + V + X * (ds[0] - 1)
+            aff(vw(wn, a, a + X * len(ds)), vw(b, 0, X * len(ds)))
+
+    for h in range(2):
+        for q in range(2):
+            a = 1024 * h + 512 * q
+            aff(vw("WE", a, a + 512), ind("W0", vw("vidu", 32 * q, 32 * q + 32), PAD + 1024 * h, PAD + 1024 * h + 1024), 1.0, EPS)
+            sums([("WE", "oselb")], h, 0, q)
+        vote(1, h, False)
+    ghosts("W0")
+    for h in range(2):
+        ts(vw("TK", PAD + 1024 * h, PAD + 1024 * h + 1024), vw("KG", 1024 * h, 1024 * h + 1024), float(OFF) - TWO24, ALU.add)
+
+    for e in range(EP):
+        wn, wx = "W%d" % (e % 2), "W%d" % ((e + 1) % 2)
+        last = e == EP - 1
+        for h in range(2):
+            select(e, 1, h, wn)
+            for hole in range(2):
+                cp(vw("bu%d" % h, 64 * hole, 64 * hole + 64), vw("bb%d" % h, 64 * hole, 64 * hole + 64))
+            tt(wk(h, 1), vw("bb%d" % h, 64, 128), vw("bb%d" % h, 0, 64), ALU.subtract)
+            act(vw("junk%d" % h), wk(h, 1), ACTF.Abs, acc=vw("XS%d" % (2 + h), 64, 65))
+        for h in range(2):
+            for hole in range(2):
+                for q in range(2):
+                    a = 1024 * h + 512 * q
+                    m, we = vw("M%d" % hole, a, a + 512), vw("WE", a, a + 512)
+                    src = ind(wn, vw("bu%d" % h, 64 * hole + 32 * q, 64 * hole + 32 * q + 32))
+                    if (h, hole, q) in ON_SCALAR:
+                        act(m, src, ACTF.Identity)
+                        b = bank()
+                        mm([(vw(b), vw("pbig", 0, 128), we, True, False), (vw(b), vw("idn"), m, False, True)])
+                        act(vw("RL", a, a + 512), vw(b), ACTF.Relu)
+                        sums([("WE", "oselb"), ("RL", "oseln")], h, hole, q)
+                    else:
+                        tt(m, src, we, ALU.min)
+                        sums([("M%d" % hole, "oselb")], h, hole, q)
+            vote(2, h, False)
+            aff(wk(h, 2), wk(h, 1), sc(h, 1))
+            tt(wk(h, 3), wk(h, 2), vw("bb%d" % h, 0, 64), ALU.add)
+            cp(vw("xu", 64 * h, 64 * h + 64), wk(h, 3))
+            for q in range(2):
+                a = 1024 * h + 512 * q
+                aff(vw("KX", a, a + 512), ind("TK", vw("xu", 64 * h + 32 * q, 64 * h + 32 * q + 32)))
+            aff(sc(h, 4), sc(h, 1), 4095.0, 1.0)
+            aff(sc(h, 5), sc(h, 1), -4095.0, 4096.0)
+            tt(wk(h, 4), wk(h, 3), vid(h), ALU.is_equal)
+            aff(wk(h, 5), wk(h, 4), float(WIN - 1))
+            tt(wk(h, 6), wk(h, 5), wk(h, 3), ALU.max)
+            tt(wk(h, 7), vw("bb%d" % h, 64, 128), wk(h, 2), ALU.subtract)
+            aff(wk(h, 8), wk(h, 7), sc(h, 2))
+        for h in range(2):
+            select(e, 2, h, wn)
+            lvh = vw("lv", 64 * h, 64 * h + 64)
+            for q in range(2):
+                a = PAD + 1024 * h + 512 * q
+                aff(vw("NL", a, a + 512), spread(lvh, "repb", q), -1.0, 1.0)
+            tt(wk(h, 17), wk(h, 6), lvh, ALU.mult)
+            cp(vw("du", 64 * h, 64 * h + 64), wk(h, 17))
+            lk, rk = vw("lr%d" % h, 0, 64), vw("lr%d" % h, 64, 128)
+            ts(wk(h, 9), rk, sc(h, 3), ALU.mult)
+            tt(wk(h, 10), wk(h, 9), wk(h, 8), ALU.add)
+            tt(vw("EE%d" % h, 0, 64), lk, vid(h), ALU.subtract)
+            tt(vw("EE%d" % h, 64, 128), wk(h, 10), vid(h), ALU.subtract)
+            ts(wk(h, 11), lk, sc(h, 4), ALU.mult)
+            aff(wk(h, 12), wk(h, 10), sc(h, 5))
+            tt(wk(h, 13), wk(h, 11), wk(h, 12), ALU.add)
+            aff(wk(h, 23), wk(h, 13), -1.0, float(OFF))
+        for h in range(2):
+            for q in range(2):
+                a = 1024 * h + 512 * q
+                aff(vw("DG", a, a + 512), ind("NL", vw("du", 64 * h + 32 * q, 64 * h + 32 * q + 32)))
+        for h in range(2):
+            go = vw("PA%d" % h, 0, 64)
+            mm([(go, vw("ext", 128 * i, 128 * i + 128), vw("DG", 1024 * h + i, 1024 * h + 1024, 16), i == 0, i == 15) for i in range(16)])
+            for q in range(2):
+                c = (64 * q, 64 * q + 64)
+                tt(vw("FF%d" % h, *c), vw("EE%d" % h, *c), go, ALU.mult)
+                tt(vw("LL%d" % h, *c), vw("FF%d" % h, *c), vid(h), ALU.add)
+                cp(vw("lu%d" % h, *c), vw("LL%d" % h, *c))
+            acc, xx = vw("AA", 64 * h, 64 * h + 64), wk(h, 14)
+            tt(xx, wk(h, 23), go, ALU.mult)
+            if e == 0:
+                aff(wk(h, 19), go, -TWO24, TWO24)
+            else:
+                aff(wk(h, 18), go, -1.0, 1.0)
+                tt(wk(h, 19), acc, wk(h, 18), ALU.mult)
+            tt(acc, wk(h, 19), xx, ALU.add)
+            if not last:
+                aff(wk(h, 20), go, 2.0 * TWO24 + OFF * (TWO24 if e else 1.0), -2.0 * TWO24)
+                if e == 1:
+                    aff(wk(h, 21), xx, TWO24)
+                tt(wk(h, 15), wk(h, 20), wk(h, 21) if e == 1 else xx, ALU.subtract)
+                for q in range(2):
+                    a = PAD + 1024 * h + 512 * q
+                    tt(vw("TK", a, a + 512), vw("TK", a, a + 512), spread(wk(h, 15), "repf", q), ALU.max)
+        if last:
+            b = bank()
+            mm([(vw(b, 0, 128), vw("AA"), vw("idf"), True, True)])
+            aff(vw("AT"), vw(b, 0, 128))
+            aff(vw("LA", 16 * rank, 16 * rank + 16), vw(b, 16 * rank, 16 * rank + 16))
+            land = [vw("LA", 16 * r, 16 * r + 16) for r in peers]
+            exchange(lambda r: vw("AT", 16 * r, 16 * r + 16), vw("LA", 16 * rank, 16 * rank + 16), land, 20000)
+        for h in range(2):
+            for q in range(2):
+                a = 1024 * h + 512 * q
+                aff(vw("GA", a, a + 512), ind(wn, vw("lu%d" % h, 32 * q, 32 * q + 32)), 1.0, 3071.5)
+                tt(vw("S16", a, a + 512), ind(wn, vw("lu%d" % h, 64 + 32 * q, 96 + 32 * q)), vw("GA", a, a + 512), ALU.add)
+                if not last:
+                    sums([("S16", "oselh")], h, 0, q)
+            if not last:
+                vote(1, h, True)
+            for q in range(2):
+                b = bank()
+                mm([(vw(b, 64 * u, 64 * u + 64), vw("idh"), vw("S16", 1024 * h + part_of(8 * q + u), 1024 * h + 1024, 16), True, True) for u in range(8)])
+                a = 1024 * h + 512 * q
+                aff(vw("WO", a, a + 512) if last else vw(wx, PAD + a, PAD + a + 512), vw(b), 0.5, -1536.0)
+            if not last:
+                ts(vw("WE", 1024 * h, 1024 * h + 1024), vw("S16", 1024 * h, 1024 * h + 1024), 0.5, ALU.mult, EPS - 1536.0, ALU.add)
+                if h == 0:
+                    ghosts(wx)
+            else:
+                cs = slice(1024 * h, 1024 * h + 1024)
+                dma("S", raw("eW%d" % h, ALL), vw("WO", 1024 * h, 1024 * h + 1024), 262144)
+                dma("S", raw("sW%d" % h, rank), vw("WO", 1024 * h, 1024 * h + 1024, 1, (16 * rank, 16 * rank + 16)), 32768)
+                exchange(lambda r, h=h: raw("eW%d" % h, r), raw("sW%d" % h, rank), [raw("sWin%d" % h, 0)], 32768)
+                dma("S", raw("yw", (ALL, cs), 0, (h, h + 1)), raw("sW%d" % h, ALL), 262144, also=raw("sWin%d" % h, 0))
+
+    b = bank()
+    mm([(vw(b, 0, 128), vw("LA"), vw("idf"), True, True)])
+    aff(vw("kvm"), vw(b, 0, 128))
+    for h in range(2):
+        for q in range(2):
+            a = 1024 * h + 512 * q
+            tt(vw("YY", a, a + 512), vw("KR", a, a + 512), spread(vw("kvm", 64 * h, 64 * h + 64), "repf", q), ALU.min)
+            act(vw("YK", a, a + 512), vw("YY", a, a + 512), ACTF.Abs)
+            dma("A", raw("yk", (ALL, slice(a, a + 512)), 0, (a, a + 512)), vw("YK", a, a + 512), 262144)
+    return ops
+
+
+def depend(ops):
+    seen = {}
+    for i, o in enumerate(ops):
+        dep = {j: True for j in o["after"]}
+        for acc, w in ((o["rd"], False), (o["wr"], True)):
+            for (name, a, b) in acc:
+                psum = name in SCRATCH and SCRATCH[name][0] == "psum"
+                for (j, a2, b2, w2) in seen.get(name, []):
+                    if j != i and a < b2 and a2 < b and (w or w2 or psum):
+                        dep[j] = dep.get(j, False) or ((w or w2) and not ("P" in o["alts"] and "P" in ops[j]["alts"]))
+        for acc, w in ((o["rd"], False), (o["wr"], True)):
+            for (name, a, b) in acc:
+                lst = seen.setdefault(name, [])
+                if w:
+                    lst[:] = [s for s in lst if not (a <= s[1] and s[2] <= b)]
+                lst.append((i, a, b, w))
+        o["dep"] = dep
+
+
+def lower(a, x):
+    lo, hi = 0, len(a)
+    while lo < hi:
+        m = (lo + hi) // 2
+        if a[m] <= x:
+            lo = m + 1
+        else:
+            hi = m
+    return lo
+
+
+def place(seq, pred, lat, eng, cost):
+    S, F = {k: [] for k in "PDASG"}, {k: [] for k in "PDASG"}
+    start, done = [0.0] * len(seq), [0.0] * len(seq)
+    for i in seq:
+        e, c, t = eng[i], cost[i], 0.0
+        for j, hard in pred[i]:
+            u = done[j] + (HOP if (hard or eng[j] != e) else 0.0)
+            if u > t:
+                t = u
+        if e != "X":
+            s, f = S[e], F[e]
+            if f and f[-1] > t:
+                k = lower(f, t)
+                while k < len(s) and t + c > s[k] + 1e-9:
+                    t = max(t, f[k])
+                    k += 1
+                s.insert(k, t)
+                f.insert(k, t + c)
+            else:
+                s.append(t)
+                f.append(t + c)
+        start[i], done[i] = t, t + c + lat[i]
+    return start, max(done)
+
+
+def improve(ops, rounds, seed=0, heat=100.0):
+    n = len(ops)
+    pred = [list(o["dep"].items()) for o in ops]
+    lat = [o["lat"] for o in ops]
+    eng = ["A" if len(o["alts"]) == 2 else list(o["alts"])[0] for o in ops]
+    cost = [o["alts"][e][1] for o, e in zip(ops, eng)]
+
+    def sequence(p):
+        p = list(p)
+        for i in range(n):
+            for j, hard in pred[i]:
+                if p[j] > p[i]:
+                    p[i] = p[j]
+        return np.argsort(np.array(p), kind="stable").tolist()
+
+    tail = [0.0] * n
+    for i in range(n - 1, -1, -1):
+        tail[i] += cost[i] + lat[i]
+        for j, hard in pred[i]:
+            tail[j] = max(tail[j], tail[i] + HOP)
+    rng = np.random.default_rng(seed)
+    start, end = place(sequence([-t for t in tail]), pred, lat, eng, cost)
+    prio, best = list(start), (end, start, eng)
+    for k in range(rounds):
+        p, e2, c2 = list(prio), list(eng), list(cost)
+        near = np.flatnonzero(np.abs(np.array(start) - rng.random() * end) < 2000.0)
+        if len(near) == 0:
+            continue
+        for i in rng.choice(near, size=min(len(near), int(rng.integers(1, 5))), replace=False).tolist():
+            if len(ops[i]["alts"]) == 2 and rng.random() < 0.4:
+                e2[i] = "A" if e2[i] == "D" else "D"
+                c2[i] = ops[i]["alts"][e2[i]][1]
+            else:
+                p[i] += rng.normal(0.0, 1500.0)
+        s, t = place(sequence(p), pred, lat, e2, c2)
+        if t <= end or rng.random() < math.exp((end - t) / (heat * (1 - k / rounds) + 1)):
+            end, start, eng, cost, prio = t, s, e2, c2, (list(s) if rng.random() < 0.1 else p)
+            if t < best[0]:
+                best = (t, s, e2)
+    return sorted(range(n), key=lambda i: (best[1][i], i)), best[2], best[1], best[0]
+
+
+def emit_all(g, T, ops, order, eng):
+    queue = {"P": g.tensor, "D": g.vector, "A": g.scalar, "S": g.sync, "G": g}
+    pos, cnt = {}, {}
+    at = {i: k for k, i in enumerate(order)}
+    for i in order:
+        if ops[i]["kind"] == "c":
+            cnt[eng[i]] = cnt.get(eng[i], 0) + 1
+            pos[i] = cnt[eng[i]]
+    know = {q: {} for q in queue}
+    clock, waits, wanted = {}, {}, set()
+    for i in order:
+        o = ops[i]
+        if o["kind"] == "a":
+            clock[i] = {("e", i): 1}
+            continue
+        k = know[eng[i]]
+        need = []
+        for j in sorted(o["dep"], key=lambda j: -at[j]):
+            p = ops[j]
+            if p["kind"] == "s":
+                continue
+            if p["kind"] == "c":
+                if eng[j] == eng[i] and o["kind"] == "c" and not o["dep"][j]:
+                    continue
+                key, val = eng[j], pos[j]
+            else:
+                key, val = ("e", j), 1
+            if k.get(key, 0) >= val:
+                continue
+            need.append(j)
+            wanted.add(j)
+            for a, b in clock[j].items():
+                k[a] = max(k.get(a, 0), b)
+        waits[i] = need
+        c = dict(k)
+        if o["kind"] == "c":
+            c[eng[i]] = max(c.get(eng[i], 0), pos[i])
+        else:
+            c[("e", i)] = 1
+        clock[i] = c
+    sem, tick, nd, ns = {}, {}, 0, 0
+    for i in order:
+        o = ops[i]
+        if o["kind"] == "c" and i in wanted:
+            tick[eng[i]] = tick.get(eng[i], 0) + 1
+            sem[i] = ("c" + eng[i], tick[eng[i]])
+        elif o["kind"] == "d":
+            sem[i] = ("dm%d" % nd, 16)
+            nd += 1
+        elif o["kind"] == "a":
+            sem[i] = o["sem"]
+    for i in order:
+        o = ops[i]
+        if o["kind"] == "a":
+            continue
+        for j in waits[i]:
+            queue[eng[i]].wait_ge(T.sem[sem[j][0]], sem[j][1])
+        r = o["alts"][eng[i]][0](g)
+        if o["kind"] == "s":
+            ns += 1
+        elif i in sem:
+            r.then_inc(T.sem[sem[i][0]], 16 if o["kind"] == "d" else 1)
+    g.wait_ge(T.sem.sent, ns * 2 * (N - 1))
+    for i in order:
+        if ops[i]["kind"] in "da" and i not in wanted:
+            g.wait_ge(T.sem[sem[i][0]], sem[i][1])
+
+
+PLAN = {"rounds": 24000}
+
+
+def rank_program(g, core, T, topo):
+    rank = T.rank_of(core)
+    if rank is None:
+        return
+    ops = build(rank, T, topo)
+    depend(ops)
+    if "order" not in PLAN:
+        PLAN["order"], PLAN["eng"], PLAN["start"], PLAN["end"] = improve(ops, PLAN["rounds"])
+    emit_all(g, T, ops, PLAN["order"], PLAN["eng"])

@@ -12,6 +12,8 @@ OFF = PAD * 4097
 TWO24 = float(2 ** 24)
 MAGIC = 1.5 * 2 ** 23
 EPS = 2.0 ** -11
+IN = [("w", 0, 1024), ("kids", 0, 512), ("kids", 512, 1024), ("w", 1024, 2048), ("kids", 1024, 2048)]
+OUT = [(0, 1024), (1024, 1536), (1536, 2048)]
 
 SCRATCH = {}
 SIZE = {"float32": 4, "int32": 4, "bfloat16": 2, "float16": 2, "uint16": 2}
@@ -50,11 +52,15 @@ _decl("PA0 PA1 PG0 PG1 PG2 PG3 PG4 PV", 512, "float32", "psum")
 for _h in range(2):
     SCRATCH["kt%d" % _h] = ("sbuf", [128, 8, 2, 8], "float32")
     SCRATCH["lt%d" % _h] = ("sbuf", [128, 8, 2, 8], "bfloat16")
-    for _n, _d in (("dW", "bfloat16"), ("rW", "bfloat16"), ("dK", "int32"), ("rK", "int32"), ("eW", "bfloat16"), ("sW", "bfloat16")):
-        SCRATCH["%s%d" % (_n, _h)] = ("dram", [N, 128, 128], _d)
+for _k, (_n, _a, _b) in enumerate(IN):
+    for _s in "dr":
+        SCRATCH["%si%d" % (_s, _k)] = ("dram", [N, 128, (_b - _a) // 8], "bfloat16" if _n == "w" else "int32")
+for _k, (_a, _b) in enumerate(OUT):
+    for _s in "dr":
+        SCRATCH["%so%d" % (_s, _k)] = ("dram", [N, 128, (_b - _a) // 8], "bfloat16")
 
-NDMA = 32
-SEMAPHORES = ["cP", "cD", "cA", "cG", "sent"] + ["dm%d" % k for k in range(NDMA)] + ["ar%d" % k for k in range(7)]
+NDMA = 80
+SEMAPHORES = ["cP", "cD", "cA", "cG", "sent"] + ["dm%d" % k for k in range(NDMA)] + ["ar%d" % k for k in range(len(IN) + len(OUT) + 1)]
 ALL = slice(None)
 
 
@@ -112,11 +118,12 @@ def in_psum(v):
     return SCRATCH[v[1]][0] == "psum"
 
 
-CY, PCY, HOP = 1.04, 0.6, 100.0
-ON_SCALAR = {(0, 1, 0), (0, 1, 1), (1, 1, 1)}
+GUESS = [(0.95, 0.48, 125.0, 1.45, 3.4, 2100.0, 220.0), (1.04, 0.52, 80.0, 1.56, 3.8, 2000.0, 200.0), (0.87, 0.44, 170.0, 1.35, 3.0, 2200.0, 250.0)]
+ON_SCALAR = {(0, 1, 0), (0, 1, 1), (1, 1, 0), (1, 1, 1)}
 
 
-def build(rank, T, topo):
+def build(rank, T, topo, guess):
+    CY, PCY, HOP, GF, SF, DL, DB = guess
     ops = []
 
     def add(alts, outs, ins, kind="c", lat=0.0, after=()):
@@ -135,9 +142,9 @@ def build(rank, T, topo):
     def vcost(out, ins, two=False):
         n = count(out)
         if out[0] == "i":
-            return 60 + n * 3.8 * CY
+            return 60 + n * SF * CY
         if ins[0][0] == "i":
-            return 60 + n * 1.56 * CY
+            return 60 + n * GF * CY
         f = 1.0
         if two:
             f = 1.0 if (in_psum(ins[0]) or in_psum(ins[1])) else 2.0
@@ -157,7 +164,7 @@ def build(rank, T, topo):
             if acc is None:
                 return g.scalar.activation(ap(T, out), ap(T, a), func, bias=ap(T, bias), scale=ap(T, scale))
             return g.scalar.activation(ap(T, out), ap(T, a), func, bias=ap(T, bias), scale=ap(T, scale), accum_out=ap(T, acc))
-        return (emit, 70 + count(out) * (1.56 if a[0] == "i" else 1.0) * CY)
+        return (emit, 70 + count(out) * (GF if a[0] == "i" else 1.0) * CY)
 
     def ts(out, a, s1, op0, s2=None, op1=None):
         return add({"D": ts_alt(out, a, s1, op0, s2, op1)}, [out], [a, s1, s2])
@@ -202,7 +209,7 @@ def build(rank, T, topo):
         def emit(g):
             e = g.sync if q == "S" else g.scalar
             return e.dma_start(ap(T, out), ap(T, src))
-        return add({q: (emit, 60)}, [out], [src, also], "d", 2000 + nbytes / 200.0, after)
+        return add({q: (emit, 150)}, [out], [src, also], "d", DL + nbytes / DB, after)
 
     me = T.cores[rank]
     peers = [(rank + d) % N for d in range(1, N)]
@@ -226,22 +233,21 @@ def build(rank, T, topo):
                 trs.append(RemoteDMATransfer(dst_ids=[DstId(rid=rid, pnc=pid)], dma_engine_mask=masks[r], remote_sem=T.sem["ar%d" % k],
                                              src=ap(T, src_of(r)), dst=ap(T, dst)))
             return g.remote_dma_fused(trs, local_sem=T.sem.sent)
-        s = add({"G": (emit, 300)}, [], [src_of(r) for r in peers], "s")
-        i = add({"X": (None, 0)}, land, [], "a", 2200 + nbytes / 30.0, [s])
+        s = add({"G": (emit, 500)}, [], [src_of(r) for r in peers], "s")
+        i = add({"X": (None, 0)}, land, [], "a", DL + nbytes * 7 / DB, [s])
         ops[i]["sem"] = ("ar%d" % k, 2 * (N - 1))
         return i
 
     rows = slice(16 * rank, 16 * rank + 16)
-    first = {}
-    for h in range(2):
-        cs = slice(1024 * h, 1024 * h + 1024)
-        for src, k, to, at, nb in (("w", "W", "W0", PAD, 262144), ("kids", "K", "KG", 0, 524288)):
-            d, r = "d%s%d" % (k, h), "r%s%d" % (k, h)
-            q = "A" if (k, h) == ("K", 0) else "S"
-            first[k] = dma(q, raw(d, ALL), raw(src, (ALL, cs)), nb, [first[k]] if h else [])
-            dma(q, raw(r, rank), raw(src, (rows, cs)), nb // N, [first[k]] if h else [])
-            exchange(lambda x, d=d: raw(d, x), raw(r, rank), [raw(r + "in", 0)], nb // N)
-            ld = dma("S", vw(to, at + 1024 * h, at + 1024 * h + 1024), raw(r, ALL), nb, also=raw(r + "in", 0))
+    staged = []
+    for k, (src, a, b) in enumerate(IN):
+        d, r, cs = "di%d" % k, "ri%d" % k, slice(a, b)
+        nb = 128 * (b - a) * SIZE[SCRATCH[d][2]]
+        q, after = ("A", []) if k in (1, 2) else ("S", staged[k - 3:k - 2] if k else [])
+        staged.append(dma(q, raw(d, ALL), raw(src, (ALL, cs)), nb, after))
+        dma(q, raw(r, rank), raw(src, (rows, cs)), nb // N, after)
+        exchange(lambda x, d=d: raw(d, x), raw(r, rank), [raw(r + "in", 0)], nb // N)
+        ld = dma("S", vw("W0", PAD + a, PAD + b) if src == "w" else vw("KG", a, b), raw(r, ALL), nb, also=raw(r + "in", 0))
     dma("S", vw("KR"), raw("kids", ALL), 1048576, [ld])
 
     def P(k):
@@ -250,6 +256,7 @@ def build(rank, T, topo):
     def vid(h):
         return vw("PV", 64 * h, 64 * h + 64)
 
+    ident = vw("pbig", 0, 128)
     iota(vw("coli"), [[1, 256]], 0, 0)
     iota(vw("pi", 0, 1), [[1, 1]], 0, 1)
     AND, SHR = ALU.bitwise_and, ALU.arith_shift_right
@@ -279,7 +286,8 @@ def build(rank, T, topo):
         ms(vw(b, 0, PAD), 0.0)
     ms(vw("NL", PAD + V, WIN), 1.0)
     for k in range(4):
-        ms(vw("RB%d" % k), 0.0)
+        if k > 1:
+            ms(vw("RB%d" % k), 0.0)
         ms(vw("RF%d" % k), 0.0)
     ts(vw("ci", 0, 128), vw("coli", 0, 128), 15, AND)
     ts(vw("oselb"), vw("ci", 0, 32), P(1), ALU.is_equal)
@@ -288,7 +296,7 @@ def build(rank, T, topo):
     ts(vw("sel32"), vw("ci", 0, 128), P(1), ALU.is_equal, 32.0, ALU.mult)
     ts(vw("idf"), vw("coli", 0, 128), P(0), ALU.is_equal)
     cp(vw("idh"), vw("idf"))
-    aff(vw("pbig", 0, 128), vw("idf"))
+    aff(ident, vw("idf"))
     aff(vw("pbig", 128, 256), vw("idf"))
     aff(vw("idn"), vw("idf"), -1.0)
     ts(vw("ci", 128, 192), vw("coli", 0, 64), 4, SHR, 1, AND)
@@ -309,7 +317,7 @@ def build(rank, T, topo):
     for i in range(16):
         aff(vw("repf", 128 * i, 128 * i + 128), vw("blk"), vw("rowm", i, i + 1))
         aff(vw("repb", 128 * i, 128 * i + 128), vw("blk"), vw("rowm", i, i + 1))
-        aff(vw("ext", 128 * i, 128 * i + 128), vw("pbig", 0, 128), vw("rowm", i, i + 1))
+        aff(vw("ext", 128 * i, 128 * i + 128), ident, vw("rowm", i, i + 1))
     for j in range(N - 1):
         a = PAD + V + X * j
         ts(vw("TK", a, a + X), vw("coli"), float(a), ALU.add, 4097.0, ALU.mult)
@@ -333,8 +341,11 @@ def build(rank, T, topo):
     def spread(src, mats, q):
         b = bank()
         items = [(vw(b, 64 * u, 64 * u + 64), vw(mats, 128 * part_of(8 * q + u), 128 * part_of(8 * q + u) + 128), src, True, True) for u in range(8)]
-        mm(items[:4])
-        mm(items[4:])
+        if mats == "repf":
+            mm(items[:4])
+            mm(items[4:])
+        else:
+            mm(items)
         return vw(b)
 
     def sums(terms, h, hole, q):
@@ -356,7 +367,7 @@ def build(rank, T, topo):
             aff(vw(xs, 0, n), vw(pa, 0, n), 0.5, -64.0 * 1536)
         else:
             ts(vw(xs, 0, n), vw(pa, 0, n), MAGIC, ALU.add, MAGIC, ALU.subtract)
-        mm([(vw(pa, 0, n1), vw("pbig", 0, 128), vw("tb", 0, n1), True, False), (vw(pa, 0, n1), vw("pbig", 0, 128), vw("tm", 0, n1), False, False),
+        mm([(vw(pa, 0, n1), ident, vw("tb", 0, n1), True, False), (vw(pa, 0, n1), ident, vw("tm", 0, n1), False, False),
             (vw(pa, 0, n1), vw("sel32"), vw(xs, 0, n1), False, True)])
         red(sc(h, 0), vw(pa, 0, n))
         ts(vw("oh%d" % h, 0, n), vw(pa, 0, n), sc(h, 0), ALU.is_equal)
@@ -365,10 +376,11 @@ def build(rank, T, topo):
             above(sc(h, 2), vw(pa, 64, 65))
             aff(sc(h, 3), sc(h, 2), -1.0, 1.0)
         tr(vw("ohT%d" % h, 0, n), vw("oh%d" % h, 0, n))
-        cp(ind(rb, vw("soff", 0, 2 * t)), vw("ohT%d" % h, 0, n))
         if t == 1:
             cp(ind(rf, vw("soff", 0, 2)), vw("ohT%d" % h, 0, 32))
+            aff(vw(rb, 0, 128), vw(rf))
         else:
+            cp(ind(rb, vw("soff", 0, 4)), vw("ohT%d" % h, 0, n))
             tt(ind(rf, vw("soff", 0, 2)), vw("ohT%d" % h, 0, 32), vw("ohT%d" % h, 32, 64), ALU.add)
 
     def select(e, t, h, wn):
@@ -388,7 +400,8 @@ def build(rank, T, topo):
                 ki.append((ok, vw("KX", a, b, 8), vw(rf, i0, 128, 8), True, True))
         lvh = vw("l1" if t == 1 else "lv", 64 * h, 64 * h + 64)
         mm(wi)
-        mm(ki)
+        mm(ki[:4])
+        mm(ki[4:])
         for k in range(2):
             above(raw(lt, (ALL, ALL, k, ALL), 64, (k, k + 1)), vw(lb, 64 * k, 64 * k + 64), P(13 + 2 * t + k))
         mm([(vw(lb, 128, 192), raw(lt, (ALL, ALL, ALL, ALL), 128), vw("selnb" if t == 1 else "seljb"), True, True)])
@@ -409,9 +422,13 @@ def build(rank, T, topo):
         ts(vw(dst, 64, 128), ti, 12, SHR, 4095, AND)
 
     def ghosts(wn):
-        for q in range(4):
+        for d in range(4, N):
+            a = PAD + V + X * (d - 1)
+            for k, (to, fr) in enumerate((((16 * d, 128), (0, 128 - 16 * d)), ((0, 16 * d), (128 - 16 * d, 128)))):
+                i = dma("S", vw(wn, a, a + X, 1, to), vw(wn, PAD, PAD + X, 1, fr), 300000)
+                ops[i]["wr"] = [(wn, a + k, a + k + 1)]
+        for ds in ((1, 2), (3,)):
             b = bank()
-            ds = [d for d in (2 * q + 1, 2 * q + 2) if d < N]
             mm([(vw(b, X * k, X * k + X), vw("pbig", 128 - 16 * d, 256 - 16 * d), vw(wn, PAD, PAD + X), True, True) for k, d in enumerate(ds)])
             a = PAD + V + X * (ds[0] - 1)
             aff(vw(wn, a, a + X * len(ds)), vw(b, 0, X * len(ds)))
@@ -423,16 +440,15 @@ def build(rank, T, topo):
             sums([("WE", "oselb")], h, 0, q)
         vote(1, h, False)
     ghosts("W0")
-    for h in range(2):
-        ts(vw("TK", PAD + 1024 * h, PAD + 1024 * h + 1024), vw("KG", 1024 * h, 1024 * h + 1024), float(OFF) - TWO24, ALU.add)
+    for a in range(0, V, 512):
+        ts(vw("TK", PAD + a, PAD + a + 512), vw("KG", a, a + 512), float(OFF) - TWO24, ALU.add)
 
     for e in range(EP):
         wn, wx = "W%d" % (e % 2), "W%d" % ((e + 1) % 2)
         last = e == EP - 1
         for h in range(2):
             select(e, 1, h, wn)
-            for hole in range(2):
-                cp(vw("bu%d" % h, 64 * hole, 64 * hole + 64), vw("bb%d" % h, 64 * hole, 64 * hole + 64))
+            cp(vw("bu%d" % h), vw("bb%d" % h))
             tt(wk(h, 1), vw("bb%d" % h, 64, 128), vw("bb%d" % h, 0, 64), ALU.subtract)
             act(vw("junk%d" % h), wk(h, 1), ACTF.Abs, acc=vw("XS%d" % (2 + h), 64, 65))
         for h in range(2):
@@ -444,7 +460,7 @@ def build(rank, T, topo):
                     if (h, hole, q) in ON_SCALAR:
                         act(m, src, ACTF.Identity)
                         b = bank()
-                        mm([(vw(b), vw("pbig", 0, 128), we, True, False), (vw(b), vw("idn"), m, False, True)])
+                        mm([(vw(b), ident, we, True, False), (vw(b), vw("idn"), m, False, True)])
                         act(vw("RL", a, a + 512), vw(b), ACTF.Relu)
                         sums([("WE", "oselb"), ("RL", "oseln")], h, hole, q)
                     else:
@@ -457,8 +473,8 @@ def build(rank, T, topo):
             for q in range(2):
                 a = 1024 * h + 512 * q
                 aff(vw("KX", a, a + 512), ind("TK", vw("xu", 64 * h + 32 * q, 64 * h + 32 * q + 32)))
-            aff(sc(h, 4), sc(h, 1), 4095.0, 1.0)
-            aff(sc(h, 5), sc(h, 1), -4095.0, 4096.0)
+            aff(sc(h, 4), sc(h, 1), -4095.0, -1.0)
+            aff(sc(h, 5), sc(h, 1), 4095.0, -4096.0)
             tt(wk(h, 4), wk(h, 3), vid(h), ALU.is_equal)
             aff(wk(h, 5), wk(h, 4), float(WIN - 1))
             tt(wk(h, 6), wk(h, 5), wk(h, 3), ALU.max)
@@ -478,9 +494,8 @@ def build(rank, T, topo):
             tt(vw("EE%d" % h, 0, 64), lk, vid(h), ALU.subtract)
             tt(vw("EE%d" % h, 64, 128), wk(h, 10), vid(h), ALU.subtract)
             ts(wk(h, 11), lk, sc(h, 4), ALU.mult)
-            aff(wk(h, 12), wk(h, 10), sc(h, 5))
-            tt(wk(h, 13), wk(h, 11), wk(h, 12), ALU.add)
-            aff(wk(h, 23), wk(h, 13), -1.0, float(OFF))
+            aff(wk(h, 12), wk(h, 10), sc(h, 5), float(OFF))
+            tt(wk(h, 23), wk(h, 11), wk(h, 12), ALU.add)
         for h in range(2):
             for q in range(2):
                 a = 1024 * h + 512 * q
@@ -525,21 +540,23 @@ def build(rank, T, topo):
                     sums([("S16", "oselh")], h, 0, q)
             if not last:
                 vote(1, h, True)
-            for q in range(2):
+            for u0, u1 in (((0, 4), (4, 8), (8, 16)) if (h == 0 and not last) else ((0, 8), (8, 16))):
                 b = bank()
-                mm([(vw(b, 64 * u, 64 * u + 64), vw("idh"), vw("S16", 1024 * h + part_of(8 * q + u), 1024 * h + 1024, 16), True, True) for u in range(8)])
-                a = 1024 * h + 512 * q
-                aff(vw("WO", a, a + 512) if last else vw(wx, PAD + a, PAD + a + 512), vw(b), 0.5, -1536.0)
+                mm([(vw(b, 64 * (u - u0), 64 * (u - u0) + 64), vw("idh"), vw("S16", 1024 * h + part_of(u), 1024 * h + 1024, 16), True, True)
+                    for u in range(u0, u1)])
+                a, n = 1024 * h + 64 * u0, 64 * (u1 - u0)
+                aff(vw("WO", a, a + n) if last else vw(wx, PAD + a, PAD + a + n), vw(b, 0, n), 0.5, -1536.0)
             if not last:
                 ts(vw("WE", 1024 * h, 1024 * h + 1024), vw("S16", 1024 * h, 1024 * h + 1024), 0.5, ALU.mult, EPS - 1536.0, ALU.add)
                 if h == 0:
                     ghosts(wx)
-            else:
-                cs = slice(1024 * h, 1024 * h + 1024)
-                dma("S", raw("eW%d" % h, ALL), vw("WO", 1024 * h, 1024 * h + 1024), 262144)
-                dma("S", raw("sW%d" % h, rank), vw("WO", 1024 * h, 1024 * h + 1024, 1, (16 * rank, 16 * rank + 16)), 32768)
-                exchange(lambda r, h=h: raw("eW%d" % h, r), raw("sW%d" % h, rank), [raw("sWin%d" % h, 0)], 32768)
-                dma("S", raw("yw", (ALL, cs), 0, (h, h + 1)), raw("sW%d" % h, ALL), 262144, also=raw("sWin%d" % h, 0))
+
+    for k, (a, b) in enumerate(OUT):
+        d, r, nb = "do%d" % k, "ro%d" % k, 256 * (b - a)
+        dma("S", raw(d, ALL), vw("WO", a, b), nb)
+        dma("S", raw(r, rank), vw("WO", a, b, 1, (16 * rank, 16 * rank + 16)), nb // N)
+        exchange(lambda x, d=d: raw(d, x), raw(r, rank), [raw(r + "in", 0)], nb // N)
+        dma("S", raw("yw", (ALL, slice(a, b)), 0, (a, b)), raw(r, ALL), nb, also=raw(r + "in", 0))
 
     b = bank()
     mm([(vw(b, 0, 128), vw("LA"), vw("idf"), True, True)])
@@ -583,13 +600,13 @@ def lower(a, x):
     return lo
 
 
-def place(seq, pred, lat, eng, cost):
+def place(seq, pred, lat, eng, cost, hop):
     S, F = {k: [] for k in "PDASG"}, {k: [] for k in "PDASG"}
     start, done = [0.0] * len(seq), [0.0] * len(seq)
     for i in seq:
-        e, c, t = eng[i], cost[i], 0.0
+        e, c, t = eng[i], cost[i][e_of(eng, i)], 0.0
         for j, hard in pred[i]:
-            u = done[j] + (HOP if (hard or eng[j] != e) else 0.0)
+            u = done[j] + (hop if (hard or eng[j] != e) else 0.0)
             if u > t:
                 t = u
         if e != "X":
@@ -608,12 +625,34 @@ def place(seq, pred, lat, eng, cost):
     return start, max(done)
 
 
-def improve(ops, rounds, seed=0, heat=100.0):
+def e_of(eng, i):
+    return eng[i]
+
+
+def replay(order, pred, lat, eng, cost, hop):
+    free, done = {k: 0.0 for k in "PDASGX"}, [0.0] * len(order)
+    for i in order:
+        e = eng[i]
+        t = free[e]
+        for j, hard in pred[i]:
+            u = done[j] + (hop if (hard or eng[j] != e) else 0.0)
+            if u > t:
+                t = u
+        t += cost[i][e]
+        if e != "X":
+            free[e] = t
+        done[i] = t + lat[i]
+    return max(done)
+
+
+def improve(versions, rounds, seed=0):
+    ops = versions[0]
     n = len(ops)
     pred = [list(o["dep"].items()) for o in ops]
-    lat = [o["lat"] for o in ops]
+    lats = [[o["lat"] for o in v] for v in versions]
+    costs = [[{e: c for e, (f, c) in o["alts"].items()} for o in v] for v in versions]
+    hops = [g[2] for g in GUESS]
     eng = ["A" if len(o["alts"]) == 2 else list(o["alts"])[0] for o in ops]
-    cost = [o["alts"][e][1] for o, e in zip(ops, eng)]
 
     def sequence(p):
         p = list(p)
@@ -623,31 +662,40 @@ def improve(ops, rounds, seed=0, heat=100.0):
                     p[i] = p[j]
         return np.argsort(np.array(p), kind="stable").tolist()
 
+    def value(s, e, t, wide):
+        if not wide:
+            return t
+        o = np.argsort(np.array(s), kind="stable").tolist()
+        return (t + sum(replay(o, pred, lats[k], e, costs[k], hops[k]) for k in (1, 2))) / 3
+
     tail = [0.0] * n
     for i in range(n - 1, -1, -1):
-        tail[i] += cost[i] + lat[i]
+        tail[i] += costs[0][i][eng[i]] + lats[0][i]
         for j, hard in pred[i]:
-            tail[j] = max(tail[j], tail[i] + HOP)
+            tail[j] = max(tail[j], tail[i] + hops[0])
     rng = np.random.default_rng(seed)
-    start, end = place(sequence([-t for t in tail]), pred, lat, eng, cost)
-    prio, best = list(start), (end, start, eng)
-    for k in range(rounds):
-        p, e2, c2 = list(prio), list(eng), list(cost)
-        near = np.flatnonzero(np.abs(np.array(start) - rng.random() * end) < 2000.0)
-        if len(near) == 0:
-            continue
-        for i in rng.choice(near, size=min(len(near), int(rng.integers(1, 5))), replace=False).tolist():
-            if len(ops[i]["alts"]) == 2 and rng.random() < 0.4:
-                e2[i] = "A" if e2[i] == "D" else "D"
-                c2[i] = ops[i]["alts"][e2[i]][1]
-            else:
-                p[i] += rng.normal(0.0, 1500.0)
-        s, t = place(sequence(p), pred, lat, e2, c2)
-        if t <= end or rng.random() < math.exp((end - t) / (heat * (1 - k / rounds) + 1)):
-            end, start, eng, cost, prio = t, s, e2, c2, (list(s) if rng.random() < 0.1 else p)
-            if t < best[0]:
-                best = (t, s, e2)
-    return sorted(range(n), key=lambda i: (best[1][i], i)), best[2], best[1], best[0]
+    start, end = place(sequence([-t for t in tail]), pred, lats[0], eng, costs[0], hops[0])
+    for wide, (many, heat) in enumerate(rounds):
+        prio, val = list(start), value(start, eng, end, wide)
+        best = (val, start, eng, end)
+        for k in range(many):
+            p, e2 = list(prio), list(eng)
+            near = np.flatnonzero(np.abs(np.array(start) - rng.random() * end) < 2000.0)
+            if len(near) == 0:
+                continue
+            for i in rng.choice(near, size=min(len(near), int(rng.integers(1, 5))), replace=False).tolist():
+                if len(ops[i]["alts"]) == 2 and rng.random() < 0.4:
+                    e2[i] = "A" if e2[i] == "D" else "D"
+                else:
+                    p[i] += rng.normal(0.0, 1500.0)
+            s, t = place(sequence(p), pred, lats[0], e2, costs[0], hops[0])
+            v = value(s, e2, t, wide)
+            if v <= val or rng.random() < math.exp((val - v) / (heat * (1 - k / many) + 1)):
+                val, end, start, eng, prio = v, t, s, e2, (list(s) if rng.random() < 0.1 else p)
+                if v < best[0]:
+                    best = (v, s, e2, t)
+        val, start, eng, end = best
+    return sorted(range(n), key=lambda i: (start[i], i)), eng, start, val
 
 
 def emit_all(g, T, ops, order, eng):
@@ -718,15 +766,16 @@ def emit_all(g, T, ops, order, eng):
             g.wait_ge(T.sem[sem[i][0]], sem[i][1])
 
 
-PLAN = {"rounds": 24000}
+PLAN = {"rounds": [(14000, 100.0), (12000, 40.0)]}
 
 
 def rank_program(g, core, T, topo):
     rank = T.rank_of(core)
     if rank is None:
         return
-    ops = build(rank, T, topo)
+    ops = build(rank, T, topo, GUESS[0])
     depend(ops)
     if "order" not in PLAN:
-        PLAN["order"], PLAN["eng"], PLAN["start"], PLAN["end"] = improve(ops, PLAN["rounds"])
+        versions = [ops] + [build(rank, T, topo, x) for x in GUESS[1:]]
+        PLAN["order"], PLAN["eng"], PLAN["start"], PLAN["end"] = improve(versions, PLAN["rounds"])
     emit_all(g, T, ops, PLAN["order"], PLAN["eng"])

import math
import numpy as np
from concourse.bass import DstId, RemoteDMATransfer
from concourse.mybir import AluOpType, AxisListType, ActivationFunctionType

ALU = AluOpType
ACTF = ActivationFunctionType
N, V, X, EP = 8, 2048, 256, 3
PAD = 16
WIN = PAD + V + (N - 1) * X
OFF = PAD * 4097
TWO24 = float(2 ** 24)
MAGIC = 1.5 * 2 ** 23
EPS = 2.0 ** -11
IN = [("w", 0, 1024), ("kids", 0, 512), ("kids", 512, 1024), ("w", 1024, 2048), ("kids", 1024, 2048)]
OUT = [(0, 1024), (1024, 1536), (1536, 2048)]

SCRATCH = {}
SIZE = {"float32": 4, "int32": 4, "bfloat16": 2, "float16": 2, "uint16": 2}


def _decl(names, cols, dtype, where="sbuf"):
    for n in names.split():
        SCRATCH[n] = (where, [128, cols], dtype)


_decl("W0 W1 NL", WIN, "bfloat16")
_decl("TK", WIN, "float32")
_decl("KG KR", V, "int32")
_decl("WE M0 M1 RL DG WO repb ext", V, "bfloat16")
_decl("KX GA YY YK repf", V, "float32")
_decl("S16", V, "float16")
_decl("coli ci", 256, "int32")
_decl("pi", 16, "int32")
_decl("pf", 24, "float32")
_decl("rowm sc0 sc1", 16, "float32")
_decl("pbig RB0 RB1 RB2 RB3", 256, "bfloat16")
_decl("idh", 128, "float16")
_decl("oselh", 32, "float16")
_decl("oselb oseln", 32, "bfloat16")
_decl("idf blk sel32 RF0 RF1 RF2 RF3 AA AT LA kvm vid EE0 EE1 FF0 FF1 LL0 LL1", 128, "float32")
_decl("seln selj oh0 oh1 ohT0 ohT1 junk0 junk1", 64, "float32")
_decl("tb tm", 80, "bfloat16")
_decl("XS0 XS1 XS2 XS3", 80, "float32")
_decl("bb0 bb1 lr0 lr1 ti0 ti1", 128, "int32")
_decl("wk0 wk1", 1536, "float32")
_decl("lv l1 idn", 128, "bfloat16")
_decl("selnb seljb", 64, "bfloat16")
_decl("vidu bu0 bu1 lu0 lu1 xu du", 128, "uint16")
_decl("soff", 4, "uint16")
_decl("PA0 PA1 PG0 PG1 PG2 PG3 PG4 PV", 512, "float32", "psum")
for _h in range(2):
    SCRATCH["kt%d" % _h] = ("sbuf", [128, 8, 2, 8], "float32")
    SCRATCH["lt%d" % _h] = ("sbuf", [128, 8, 2, 8], "bfloat16")
for _k, (_n, _a, _b) in enumerate(IN):
    for _s in "dr":
        SCRATCH["%si%d" % (_s, _k)] = ("dram", [N, 128, (_b - _a) // 8], "bfloat16" if _n == "w" else "int32")
for _k, (_a, _b) in enumerate(OUT):
    for _s in "dr":
        SCRATCH["%so%d" % (_s, _k)] = ("dram", [N, 128, (_b - _a) // 8], "bfloat16")

NDMA = 80
SEMAPHORES = ["cP", "cD", "cA", "cG", "sent"] + ["dm%d" % k for k in range(NDMA)] + ["ar%d" % k for k in range(len(IN) + len(OUT) + 1)]
ALL = slice(None)


def vw(name, a=0, b=None, s=1, p=None):
    if b is None:
        b = SCRATCH[name][1][-1]
    return ("v", name, a, b, s, p)


def ind(name, offs, a=0, b=None):
    return ("i", name, offs, a, SCRATCH[name][1][-1] if b is None else b)


def raw(name, index, n=0, part=(0, 1 << 30)):
    return ("r", name, index, n, part)


def ap(T, v):
    if not isinstance(v, tuple):
        return v
    if v[0] == "v":
        rows = ALL if v[5] is None else slice(v[5][0], v[5][1])
        cols = slice(v[2], v[3]) if v[4] == 1 else slice(v[2], v[3], v[4])
        return T[v[1]][rows, cols]
    if v[0] == "i":
        return T[v[1]][:, v[3]:v[4]].indirect(ap(T, v[2]))
    return T[v[1]][v[2]]


def regions(v):
    if not isinstance(v, tuple):
        return []
    if v[0] == "v":
        if SCRATCH[v[1]][0] == "psum":
            return [(v[1], 0, 512)]
        return [(v[1], v[2], v[3])]
    if v[0] == "i":
        return [(v[1], v[3], v[4])] + regions(v[2])
    return [(v[1],) + v[4]]


def count(v):
    if v[0] == "r":
        return v[3]
    if v[0] == "i":
        return 16 * count(v[2])
    return len(range(v[2], v[3], v[4]))


def width(v):
    return SIZE[SCRATCH[v[1]][2]]


def in_psum(v):
    return SCRATCH[v[1]][0] == "psum"


GUESS = [(0.95, 0.48, 125.0, 1.45, 3.4, 2100.0, 220.0), (1.04, 0.52, 80.0, 1.56, 3.8, 2000.0, 200.0), (0.87, 0.44, 170.0, 1.35, 3.0, 2200.0, 250.0)]
ON_SCALAR = {(0, 1, 0), (0, 1, 1), (1, 1, 0), (1, 1, 1)}


def build(rank, T, topo, guess):
    CY, PCY, HOP, GF, SF, DL, DB = guess
    ops = []

    def add(alts, outs, ins, kind="c", lat=0.0, after=()):
        rd, wr = [], []
        for v in ins:
            rd += regions(v)
        for v in outs:
            if v[0] == "i":
                wr += regions(v)[:1]
                rd += regions(v)[1:]
            else:
                wr += regions(v)
        ops.append({"alts": alts, "rd": rd, "wr": wr, "kind": kind, "lat": lat, "after": list(after)})
        return len(ops) - 1

    def vcost(out, ins, two=False):
        n = count(out)
        if out[0] == "i":
            return 60 + n * SF * CY
        if ins[0][0] == "i":
            return 60 + n * GF * CY
        f = 1.0
        if two:
            f = 1.0 if (in_psum(ins[0]) or in_psum(ins[1])) else 2.0
        elif width(out) == 2 and width(ins[0]) == 2:
            f = 0.5
        return 30 + max(64, n * f) * CY

    def ts_alt(out, a, s1, op0, s2=None, op1=None):
        def emit(g):
            if op1 is None:
                return g.vector.tensor_scalar(ap(T, out), ap(T, a), ap(T, s1), None, op0)
            return g.vector.tensor_scalar(ap(T, out), ap(T, a), ap(T, s1), ap(T, s2), op0, op1)
        return (emit, vcost(out, [a]))

    def act_alt(out, a, func, scale, bias, acc):
        def emit(g):
            if acc is None:
                return g.scalar.activation(ap(T, out), ap(T, a), func, bias=ap(T, bias), scale=ap(T, scale))
            return g.scalar.activation(ap(T, out), ap(T, a), func, bias=ap(T, bias), scale=ap(T, scale), accum_out=ap(T, acc))
        return (emit, 70 + count(out) * (GF if a[0] == "i" else 1.0) * CY)

    def ts(out, a, s1, op0, s2=None, op1=None):
        return add({"D": ts_alt(out, a, s1, op0, s2, op1)}, [out], [a, s1, s2])

    def act(out, a, func, scale=1.0, bias=0.0, acc=None):
        return add({"A": act_alt(out, a, func, scale, bias, acc)}, [out] + ([acc] if acc else []), [a, scale, bias])

    def aff(out, a, scale=1.0, bias=0.0):
        return add({"A": act_alt(out, a, ACTF.Identity, scale, bias, None), "D": ts_alt(out, a, scale, ALU.mult, bias, ALU.add)}, [out], [a, scale, bias])

    def above(out, a, scale=1.0):
        return add({"A": act_alt(out, a, ACTF.Sign, scale, 0.0, None), "D": ts_alt(out, a, scale, ALU.mult, 0.0, ALU.is_gt)}, [out], [a, scale])

    def tt(out, a, b, op):
        return add({"D": (lambda g: g.vector.tensor_tensor(ap(T, out), ap(T, a), ap(T, b), op), vcost(out, [a, b], True))}, [out], [a, b])

    def cp(out, a):
        return add({"D": (lambda g: g.vector.tensor_copy(ap(T, out), ap(T, a)), vcost(out, [a]))}, [out], [a])

    def red(out, a):
        return add({"D": (lambda g: g.vector.tensor_reduce(ap(T, out), ap(T, a), AxisListType.X, ALU.max), 30 + max(64, count(a)) * CY)}, [out], [a])

    def tr(out, a):
        return add({"D": (lambda g: g.vector.transpose(ap(T, out), ap(T, a)), vcost(out, [a]))}, [out], [a])

    def ms(out, c):
        return add({"D": (lambda g: g.vector.memset(ap(T, out), c), 30 + max(64, count(out) * width(out) / 4) * CY)}, [out], [])

    def mm(items):
        def emit(g):
            r = None
            for (o, l, x, st, sp) in items:
                r = g.tensor.matmul(ap(T, o), ap(T, l), ap(T, x), st, sp)
            return r
        c = 40 + sum(max(min(64, count(l)), count(x)) * (4 if width(x) == 4 else 1) * PCY for (o, l, x, st, sp) in items)
        return add({"P": (emit, c)}, [i[0] for i in items], [i[1] for i in items] + [i[2] for i in items])

    def iota(out, pattern, base, mult):
        return add({"G": (lambda g: g.iota(ap(T, out), pattern, base, mult), 130 + 2 * count(out) * CY)}, [out], [])

    def dma(q, out, src, nbytes, after=(), also=None):
        def emit(g):
            e = g.sync if q == "S" else g.scalar
            return e.dma_start(ap(T, out), ap(T, src))
        return add({q: (emit, 150)}, [out], [src, also], "d", DL + nbytes / DB, after)

    me = T.cores[rank]
    peers = [(rank + d) % N for d in range(1, N)]
    far = [r for r in peers if topo.die(T.cores[r]) != topo.die(me)]
    near = [r for r in peers if topo.die(T.cores[r]) == topo.die(me)]
    masks = {}
    for lst, first in ((far, 0), (near, 1)):
        for k, r in enumerate(lst):
            e = topo.engines(me, T.cores[r])[first::2]
            masks[r] = (1 << e[2 * k]) | (1 << e[2 * k + 1])
    nsend = [0]

    def exchange(src_of, dst, land, nbytes):
        k = nsend[0]
        nsend[0] += 1

        def emit(g):
            trs = []
            for r in peers:
                rid, pid, se = topo.addr(T.cores[r])
                trs.append(RemoteDMATransfer(dst_ids=[DstId(rid=rid, pnc=pid)], dma_engine_mask=masks[r], remote_sem=T.sem["ar%d" % k],
                                             src=ap(T, src_of(r)), dst=ap(T, dst)))
            return g.remote_dma_fused(trs, local_sem=T.sem.sent)
        s = add({"G": (emit, 500)}, [], [src_of(r) for r in peers], "s")
        i = add({"X": (None, 0)}, land, [], "a", DL + nbytes * 7 / DB, [s])
        ops[i]["sem"] = ("ar%d" % k, 2 * (N - 1))
        return i

    rows = slice(16 * rank, 16 * rank + 16)
    staged = []
    for k, (src, a, b) in enumerate(IN):
        d, r, cs = "di%d" % k, "ri%d" % k, slice(a, b)
        nb = 128 * (b - a) * SIZE[SCRATCH[d][2]]
        q, after = ("A", []) if k in (1, 2) else ("S", staged[k - 3:k - 2] if k else [])
        staged.append(dma(q, raw(d, ALL), raw(src, (ALL, cs)), nb, after))
        dma(q, raw(r, rank), raw(src, (rows, cs)), nb // N, after)
        exchange(lambda x, d=d: raw(d, x), raw(r, rank), [raw(r + "in", 0)], nb // N)
        ld = dma("S", vw("W0", PAD + a, PAD + b) if src == "w" else vw("KG", a, b), raw(r, ALL), nb, also=raw(r + "in", 0))
    dma("S", vw("KR"), raw("kids", ALL), 1048576, [ld])

    def P(k):
        return vw("pf", k, k + 1)

    def vid(h):
        return vw("PV", 64 * h, 64 * h + 64)

    ident = vw("pbig", 0, 128)
    iota(vw("coli"), [[1, 256]], 0, 0)
    iota(vw("pi", 0, 1), [[1, 1]], 0, 1)
    AND, SHR = ALU.bitwise_and, ALU.arith_shift_right
    spec = [None, (15, None), (None, 4), (1, 4), (63, None), (None, 6), (1, None), (None, 1), (7, None), (1, 3), (None, 5)]
    for k, sp in enumerate(spec):
        if sp is None:
            continue
        o, a = vw("pi", k, k + 1), vw("pi", 0, 1)
        if sp[1] is None:
            ts(o, a, sp[0], AND)
        elif sp[0] is None:
            ts(o, a, sp[1], SHR)
        else:
            ts(o, a, sp[1], SHR, sp[0], AND)
    cp(vw("pf", 0, 11), vw("pi", 0, 11))
    aff(P(11), P(8), 128.0, float(PAD))
    aff(P(12), P(9), 64.0, P(11))
    aff(P(14), P(9), 64.0, P(8))
    aff(P(13), P(10), 16.0, P(14))
    for k in range(2):
        ts(P(15 + k), P(5), float(k), ALU.is_equal)
        ts(P(17 + k), P(6), float(k), ALU.is_equal)
    for h in range(2):
        ts(vw("vid", 64 * h, 64 * h + 64), vw("coli", 0, 64), P(12), ALU.add, 1024.0 * h, ALU.add)
    ts(vw("vidu", 0, 64), vw("vid", 0, 64), -float(PAD), ALU.add)
    for b in ("W0", "W1", "TK", "NL"):
        ms(vw(b, 0, PAD), 0.0)
    ms(vw("NL", PAD + V, WIN), 1.0)
    for k in range(4):
        if k > 1:
            ms(vw("RB%d" % k), 0.0)
        ms(vw("RF%d" % k), 0.0)
    ts(vw("ci", 0, 128), vw("coli", 0, 128), 15, AND)
    ts(vw("oselb"), vw("ci", 0, 32), P(1), ALU.is_equal)
    ts(vw("oselh"), vw("ci", 0, 32), P(1), ALU.is_equal)
    aff(vw("oseln"), vw("oselb"), -1.0)
    ts(vw("sel32"), vw("ci", 0, 128), P(1), ALU.is_equal, 32.0, ALU.mult)
    ts(vw("idf"), vw("coli", 0, 128), P(0), ALU.is_equal)
    cp(vw("idh"), vw("idf"))
    aff(ident, vw("idf"))
    aff(vw("pbig", 128, 256), vw("idf"))
    aff(vw("idn"), vw("idf"), -1.0)
    ts(vw("ci", 128, 192), vw("coli", 0, 64), 4, SHR, 1, AND)
    ts(vw("tm", 0, 64), vw("ci", 128, 192), P(3), ALU.not_equal, -float(2 ** 23), ALU.mult)
    ts(vw("tb", 0, 32), vw("ci", 0, 32), -1.0, ALU.mult, 31.0, ALU.add)
    ts(vw("tb", 32, 64), vw("ci", 0, 32), -1.0, ALU.mult, 15.0, ALU.add)
    ms(vw("tb", 64, 80), 0.0)
    ms(vw("tm", 64, 80), 0.0)
    for cc in range(4):
        ts(vw("soff", cc, cc + 1), P(13), float(128 * (cc // 2) + 8 * (cc % 2)), ALU.add)
    ts(vw("seln"), vw("coli", 0, 64), P(4), ALU.is_equal)
    ts(vw("selj"), vw("coli", 0, 64), P(7), ALU.is_equal)
    aff(vw("selnb"), vw("seln"))
    aff(vw("seljb"), vw("selj"))
    ts(vw("ti1"), vw("coli", 0, 128), 4, SHR)
    ts(vw("blk"), vw("ti1"), P(2), ALU.is_equal)
    ts(vw("rowm"), vw("coli", 0, 16), P(1), ALU.is_equal)
    for i in range(16):
        aff(vw("repf", 128 * i, 128 * i + 128), vw("blk"), vw("rowm", i, i + 1))
        aff(vw("repb", 128 * i, 128 * i + 128), vw("blk"), vw("rowm", i, i + 1))
        aff(vw("ext", 128 * i, 128 * i + 128), ident, vw("rowm", i, i + 1))
    for j in range(N - 1):
        a = PAD + V + X * j
        ts(vw("TK", a, a + X), vw("coli"), float(a), ALU.add, 4097.0, ALU.mult)
    mm([(vw("PV", 0, 128), vw("idf"), vw("vid"), True, True)])

    big = [0]

    def bank():
        big[0] += 1
        return "PG%d" % (big[0] % 5)

    def part_of(kk):
        return kk // 2 + 8 * (kk % 2)

    def wk(h, k):
        return vw("wk%d" % h, 64 * k, 64 * k + 64)

    def sc(h, k):
        return vw("sc%d" % h, k, k + 1)

    def spread(src, mats, q):
        b = bank()
        items = [(vw(b, 64 * u, 64 * u + 64), vw(mats, 128 * part_of(8 * q + u), 128 * part_of(8 * q + u) + 128), src, True, True) for u in range(8)]
        if mats == "repf":
            mm(items[:4])
            mm(items[4:])
        else:
            mm(items)
        return vw(b)

    def sums(terms, h, hole, q):
        o = vw("PA%d" % h, 32 * hole, 32 * hole + 32)
        items = []
        for b in range(4 * q, 4 * q + 4):
            for k, (data, osel) in enumerate(terms):
                a = 1024 * h + 128 * b
                items.append((o, vw(data, a, a + 128), vw(osel), b == 0 and k == 0, b == 7 and k == len(terms) - 1))
        mm(items)

    def vote(t, h, exact):
        n = 32 * t
        n1 = n + (t - 1)
        xs = "XS%d" % (2 * (t - 1) + h)
        rb, rf = "RB%d" % (2 * (t - 1) + h), "RF%d" % (2 * (t - 1) + h)
        pa = "PA%d" % h
        if exact:
            aff(vw(xs, 0, n), vw(pa, 0, n), 0.5, -64.0 * 1536)
        else:
            ts(vw(xs, 0, n), vw(pa, 0, n), MAGIC, ALU.add, MAGIC, ALU.subtract)
        mm([(vw(pa, 0, n1), ident, vw("tb", 0, n1), True, False), (vw(pa, 0, n1), ident, vw("tm", 0, n1), False, False),
            (vw(pa, 0, n1), vw("sel32"), vw(xs, 0, n1), False, True)])
        red(sc(h, 0), vw(pa, 0, n))
        ts(vw("oh%d" % h, 0, n), vw(pa, 0, n), sc(h, 0), ALU.is_equal)
        if t == 2:
            red(sc(h, 1), vw("oh%d" % h, 32, 64))
            above(sc(h, 2), vw(pa, 64, 65))
            aff(sc(h, 3), sc(h, 2), -1.0, 1.0)
        tr(vw("ohT%d" % h, 0, n), vw("oh%d" % h, 0, n))
        if t == 1:
            cp(ind(rf, vw("soff", 0, 2)), vw("ohT%d" % h, 0, 32))
            aff(vw(rb, 0, 128), vw(rf))
        else:
            cp(ind(rb, vw("soff", 0, 4)), vw("ohT%d" % h, 0, n))
            tt(ind(rf, vw("soff", 0, 2)), vw("ohT%d" % h, 0, 32), vw("ohT%d" % h, 32, 64), ALU.add)

    def select(e, t, h, wn):
        rb, rf = "RB%d" % (2 * (t - 1) + h), "RF%d" % (2 * (t - 1) + h)
        pa, kt, lt, lb = "PA%d" % h, "kt%d" % h, "lt%d" % h, bank()
        wi, ki = [], []
        for i0 in range(8):
            ow, ok = vw(lb, i0, 128, 8), vw(pa, i0, 128, 8)
            if t == 1:
                a = PAD + 1024 * h + 128 * i0
                wi.append((ow, vw(wn, a, a + 128), vw(rb, i0, 128, 8), True, True))
                ki.append((ok, vw("TK", a, a + 128), vw(rf, i0, 128, 8), True, True))
            else:
                a, b = 1024 * h + i0, 1024 * h + 1024
                wi.append((ow, vw("M0", a, b, 8), vw(rb, i0, 128, 8), True, False))
                wi.append((ow, vw("M1", a, b, 8), vw(rb, 128 + i0, 256, 8), False, True))
                ki.append((ok, vw("KX", a, b, 8), vw(rf, i0, 128, 8), True, True))
        lvh = vw("l1" if t == 1 else "lv", 64 * h, 64 * h + 64)
        mm(wi)
        mm(ki[:4])
        mm(ki[4:])
        for k in range(2):
            above(raw(lt, (ALL, ALL, k, ALL), 64, (k, k + 1)), vw(lb, 64 * k, 64 * k + 64), P(13 + 2 * t + k))
        mm([(vw(lb, 128, 192), raw(lt, (ALL, ALL, ALL, ALL), 128), vw("selnb" if t == 1 else "seljb"), True, True)])
        aff(lvh, vw(lb, 128, 192))
        for k in range(2):
            aff(raw(kt, (ALL, ALL, k, ALL), 64, (k, k + 1)), vw(pa, 64 * k, 64 * k + 64), P(13 + 2 * t + k))
        kp = vw(pa, 256, 320)
        mm([(kp, raw(kt, (ALL, ALL, ALL, ALL), 128), vw("seln" if t == 1 else "selj"), True, True)])
        ti = vw("ti%d" % h, 64 * (t - 1), 64 * t)
        if e == 2:
            ts(wk(h, 0), kp, TWO24, ALU.is_lt, 1.0 / TWO24, ALU.max)
            tt(wk(h, 16), wk(h, 0), lvh, ALU.mult)
            tt(ti, kp, wk(h, 16), ALU.mult)
        else:
            tt(ti, kp, lvh, ALU.mult)
        dst = ("bb%d" if t == 1 else "lr%d") % h
        ts(vw(dst, 0, 64), ti, 4095, AND)
        ts(vw(dst, 64, 128), ti, 12, SHR, 4095, AND)

    def ghosts(wn):
        for d in range(4, N):
            a = PAD + V + X * (d - 1)
            for k, (to, fr) in enumerate((((16 * d, 128), (0, 128 - 16 * d)), ((0, 16 * d), (128 - 16 * d, 128)))):
                i = dma("S", vw(wn, a, a + X, 1, to), vw(wn, PAD, PAD + X, 1, fr), 300000)
                ops[i]["wr"] = [(wn, a + k, a + k + 1)]
        for ds in ((1, 2), (3,)):
            b = bank()
            mm([(vw(b, X * k, X * k + X), vw("pbig", 128 - 16 * d, 256 - 16 * d), vw(wn, PAD, PAD + X), True, True) for k, d in enumerate(ds)])
            a = PAD + V + X * (ds[0] - 1)
            aff(vw(wn, a, a + X * len(ds)), vw(b, 0, X * len(ds)))

    for h in range(2):
        for q in range(2):
            a = 1024 * h + 512 * q
            aff(vw("WE", a, a + 512), ind("W0", vw("vidu", 32 * q, 32 * q + 32), PAD + 1024 * h, PAD + 1024 * h + 1024), 1.0, EPS)
            sums([("WE", "oselb")], h, 0, q)
        vote(1, h, False)
    ghosts("W0")
    for a in range(0, V, 512):
        ts(vw("TK", PAD + a, PAD + a + 512), vw("KG", a, a + 512), float(OFF) - TWO24, ALU.add)

    for e in range(EP):
        wn, wx = "W%d" % (e % 2), "W%d" % ((e + 1) % 2)
        last = e == EP - 1
        for h in range(2):
            select(e, 1, h, wn)
            cp(vw("bu%d" % h), vw("bb%d" % h))
            tt(wk(h, 1), vw("bb%d" % h, 64, 128), vw("bb%d" % h, 0, 64), ALU.subtract)
            act(vw("junk%d" % h), wk(h, 1), ACTF.Abs, acc=vw("XS%d" % (2 + h), 64, 65))
        for h in range(2):
            for hole in range(2):
                for q in range(2):
                    a = 1024 * h + 512 * q
                    m, we = vw("M%d" % hole, a, a + 512), vw("WE", a, a + 512)
                    src = ind(wn, vw("bu%d" % h, 64 * hole + 32 * q, 64 * hole + 32 * q + 32))
                    if (h, hole, q) in ON_SCALAR:
                        act(m, src, ACTF.Identity)
                        b = bank()
                        mm([(vw(b), ident, we, True, False), (vw(b), vw("idn"), m, False, True)])
                        act(vw("RL", a, a + 512), vw(b), ACTF.Relu)
                        sums([("WE", "oselb"), ("RL", "oseln")], h, hole, q)
                    else:
                        tt(m, src, we, ALU.min)
                        sums([("M%d" % hole, "oselb")], h, hole, q)
            vote(2, h, False)
            aff(wk(h, 2), wk(h, 1), sc(h, 1))
            tt(wk(h, 3), wk(h, 2), vw("bb%d" % h, 0, 64), ALU.add)
            cp(vw("xu", 64 * h, 64 * h + 64), wk(h, 3))
            for q in range(2):
                a = 1024 * h + 512 * q
                aff(vw("KX", a, a + 512), ind("TK", vw("xu", 64 * h + 32 * q, 64 * h + 32 * q + 32)))
            aff(sc(h, 4), sc(h, 1), -4095.0, -1.0)
            aff(sc(h, 5), sc(h, 1), 4095.0, -4096.0)
            tt(wk(h, 4), wk(h, 3), vid(h), ALU.is_equal)
            aff(wk(h, 5), wk(h, 4), float(WIN - 1))
            tt(wk(h, 6), wk(h, 5), wk(h, 3), ALU.max)
            tt(wk(h, 7), vw("bb%d" % h, 64, 128), wk(h, 2), ALU.subtract)
            aff(wk(h, 8), wk(h, 7), sc(h, 2))
        for h in range(2):
            select(e, 2, h, wn)
            lvh = vw("lv", 64 * h, 64 * h + 64)
            for q in range(2):
                a = PAD + 1024 * h + 512 * q
                aff(vw("NL", a, a + 512), spread(lvh, "repb", q), -1.0, 1.0)
            tt(wk(h, 17), wk(h, 6), lvh, ALU.mult)
            cp(vw("du", 64 * h, 64 * h + 64), wk(h, 17))
            lk, rk = vw("lr%d" % h, 0, 64), vw("lr%d" % h, 64, 128)
            ts(wk(h, 9), rk, sc(h, 3), ALU.mult)
            tt(wk(h, 10), wk(h, 9), wk(h, 8), ALU.add)
            tt(vw("EE%d" % h, 0, 64), lk, vid(h), ALU.subtract)
            tt(vw("EE%d" % h, 64, 128), wk(h, 10), vid(h), ALU.subtract)
            ts(wk(h, 11), lk, sc(h, 4), ALU.mult)
            aff(wk(h, 12), wk(h, 10), sc(h, 5), float(OFF))
            tt(wk(h, 23), wk(h, 11), wk(h, 12), ALU.add)
        for h in range(2):
            for q in range(2):
                a = 1024 * h + 512 * q
                aff(vw("DG", a, a + 512), ind("NL", vw("du", 64 * h + 32 * q, 64 * h + 32 * q + 32)))
        for h in range(2):
            go = vw("PA%d" % h, 0, 64)
            mm([(go, vw("ext", 128 * i, 128 * i + 128), vw("DG", 1024 * h + i, 1024 * h + 1024, 16), i == 0, i == 15) for i in range(16)])
            for q in range(2):
                c = (64 * q, 64 * q + 64)
                tt(vw("FF%d" % h, *c), vw("EE%d" % h, *c), go, ALU.mult)
                tt(vw("LL%d" % h, *c), vw("FF%d" % h, *c), vid(h), ALU.add)
                cp(vw("lu%d" % h, *c), vw("LL%d" % h, *c))
            acc, xx = vw("AA", 64 * h, 64 * h + 64), wk(h, 14)
            tt(xx, wk(h, 23), go, ALU.mult)
            if e == 0:
                aff(wk(h, 19), go, -TWO24, TWO24)
            else:
                aff(wk(h, 18), go, -1.0, 1.0)
                tt(wk(h, 19), acc, wk(h, 18), ALU.mult)
            tt(acc, wk(h, 19), xx, ALU.add)
            if not last:
                aff(wk(h, 20), go, 2.0 * TWO24 + OFF * (TWO24 if e else 1.0), -2.0 * TWO24)
                if e == 1:
                    aff(wk(h, 21), xx, TWO24)
                tt(wk(h, 15), wk(h, 20), wk(h, 21) if e == 1 else xx, ALU.subtract)
                for q in range(2):
                    a = PAD + 1024 * h + 512 * q
                    tt(vw("TK", a, a + 512), vw("TK", a, a + 512), spread(wk(h, 15), "repf", q), ALU.max)
        if last:
            b = bank()
            mm([(vw(b, 0, 128), vw("AA"), vw("idf"), True, True)])
            aff(vw("AT"), vw(b, 0, 128))
            aff(vw("LA", 16 * rank, 16 * rank + 16), vw(b, 16 * rank, 16 * rank + 16))
            land = [vw("LA", 16 * r, 16 * r + 16) for r in peers]
            exchange(lambda r: vw("AT", 16 * r, 16 * r + 16), vw("LA", 16 * rank, 16 * rank + 16), land, 20000)
        for h in range(2):
            for q in range(2):
                a = 1024 * h + 512 * q
                aff(vw("GA", a, a + 512), ind(wn, vw("lu%d" % h, 32 * q, 32 * q + 32)), 1.0, 3071.5)
                tt(vw("S16", a, a + 512), ind(wn, vw("lu%d" % h, 64 + 32 * q, 96 + 32 * q)), vw("GA", a, a + 512), ALU.add)
                if not last:
                    sums([("S16", "oselh")], h, 0, q)
            if not last:
                vote(1, h, True)
            for u0, u1 in (((0, 4), (4, 8), (8, 16)) if (h == 0 and not last) else ((0, 8), (8, 16))):
                b = bank()
                mm([(vw(b, 64 * (u - u0), 64 * (u - u0) + 64), vw("idh"), vw("S16", 1024 * h + part_of(u), 1024 * h + 1024, 16), True, True)
                    for u in range(u0, u1)])
                a, n = 1024 * h + 64 * u0, 64 * (u1 - u0)
                aff(vw("WO", a, a + n) if last else vw(wx, PAD + a, PAD + a + n), vw(b, 0, n), 0.5, -1536.0)
            if not last:
                ts(vw("WE", 1024 * h, 1024 * h + 1024), vw("S16", 1024 * h, 1024 * h + 1024), 0.5, ALU.mult, EPS - 1536.0, ALU.add)
                if h == 0:
                    ghosts(wx)

    for k, (a, b) in enumerate(OUT):
        d, r, nb = "do%d" % k, "ro%d" % k, 256 * (b - a)
        dma("S", raw(d, ALL), vw("WO", a, b), nb)
        dma("S", raw(r, rank), vw("WO", a, b, 1, (16 * rank, 16 * rank + 16)), nb // N)
        exchange(lambda x, d=d: raw(d, x), raw(r, rank), [raw(r + "in", 0)], nb // N)
        dma("S", raw("yw", (ALL, slice(a, b)), 0, (a, b)), raw(r, ALL), nb, also=raw(r + "in", 0))

    b = bank()
    mm([(vw(b, 0, 128), vw("LA"), vw("idf"), True, True)])
    aff(vw("kvm"), vw(b, 0, 128))
    for h in range(2):
        for q in range(2):
            a = 1024 * h + 512 * q
            tt(vw("YY", a, a + 512), vw("KR", a, a + 512), spread(vw("kvm", 64 * h, 64 * h + 64), "repf", q), ALU.min)
            act(vw("YK", a, a + 512), vw("YY", a, a + 512), ACTF.Abs)
            dma("A", raw("yk", (ALL, slice(a, a + 512)), 0, (a, a + 512)), vw("YK", a, a + 512), 262144)
    return ops


def depend(ops):
    seen = {}
    for i, o in enumerate(ops):
        dep = {j: True for j in o["after"]}
        for acc, w in ((o["rd"], False), (o["wr"], True)):
            for (name, a, b) in acc:
                psum = name in SCRATCH and SCRATCH[name][0] == "psum"
                for (j, a2, b2, w2) in seen.get(name, []):
                    if j != i and a < b2 and a2 < b and (w or w2 or psum):
                        dep[j] = dep.get(j, False) or ((w or w2) and not ("P" in o["alts"] and "P" in ops[j]["alts"]))
        for acc, w in ((o["rd"], False), (o["wr"], True)):
            for (name, a, b) in acc:
                lst = seen.setdefault(name, [])
                if w:
                    lst[:] = [s for s in lst if not (a <= s[1] and s[2] <= b)]
                lst.append((i, a, b, w))
        o["dep"] = dep


def lower(a, x):
    lo, hi = 0, len(a)
    while lo < hi:
        m = (lo + hi) // 2
        if a[m] <= x:
            lo = m + 1
        else:
            hi = m
    return lo


def place(seq, pred, lat, eng, cost, hop):
    S, F = {k: [] for k in "PDASG"}, {k: [] for k in "PDASG"}
    start, done = [0.0] * len(seq), [0.0] * len(seq)
    for i in seq:
        e, c, t = eng[i], cost[i][e_of(eng, i)], 0.0
        for j, hard in pred[i]:
            u = done[j] + (hop if (hard or eng[j] != e) else 0.0)
            if u > t:
                t = u
        if e != "X":
            s, f = S[e], F[e]
            if f and f[-1] > t:
                k = lower(f, t)
                while k < len(s) and t + c > s[k] + 1e-9:
                    t = max(t, f[k])
                    k += 1
                s.insert(k, t)
                f.insert(k, t + c)
            else:
                s.append(t)
                f.append(t + c)
        start[i], done[i] = t, t + c + lat[i]
    return start, max(done)


def e_of(eng, i):
    return eng[i]


def replay(order, pred, lat, eng, cost, hop):
    free, done = {k: 0.0 for k in "PDASGX"}, [0.0] * len(order)
    for i in order:
        e = eng[i]
        t = free[e]
        for j, hard in pred[i]:
            u = done[j] + (hop if (hard or eng[j] != e) else 0.0)
            if u > t:
                t = u
        t += cost[i][e]
        if e != "X":
            free[e] = t
        done[i] = t + lat[i]
    return max(done)


def improve(versions, rounds, seed=0):
    ops = versions[0]
    n = len(ops)
    pred = [list(o["dep"].items()) for o in ops]
    lats = [[o["lat"] for o in v] for v in versions]
    costs = [[{e: c for e, (f, c) in o["alts"].items()} for o in v] for v in versions]
    hops = [g[2] for g in GUESS]
    eng = ["A" if len(o["alts"]) == 2 else list(o["alts"])[0] for o in ops]

    def sequence(p):
        p = list(p)
        for i in range(n):
            for j, hard in pred[i]:
                if p[j] > p[i]:
                    p[i] = p[j]
        return np.argsort(np.array(p), kind="stable").tolist()

    def value(s, e, t, wide):
        if not wide:
            return t
        o = np.argsort(np.array(s), kind="stable").tolist()
        return (t + sum(replay(o, pred, lats[k], e, costs[k], hops[k]) for k in (1, 2))) / 3

    tail = [0.0] * n
    for i in range(n - 1, -1, -1):
        tail[i] += costs[0][i][eng[i]] + lats[0][i]
        for j, hard in pred[i]:
            tail[j] = max(tail[j], tail[i] + hops[0])
    rng = np.random.default_rng(seed)
    start, end = place(sequence([-t for t in tail]), pred, lats[0], eng, costs[0], hops[0])
    for wide, (many, heat) in enumerate(rounds):
        prio, val = list(start), value(start, eng, end, wide)
        best = (val, start, eng, end)
        for k in range(many):
            p, e2 = list(prio), list(eng)
            near = np.flatnonzero(np.abs(np.array(start) - rng.random() * end) < 2000.0)
            if len(near) == 0:
                continue
            for i in rng.choice(near, size=min(len(near), int(rng.integers(1, 5))), replace=False).tolist():
                if len(ops[i]["alts"]) == 2 and rng.random() < 0.4:
                    e2[i] = "A" if e2[i] == "D" else "D"
                else:
                    p[i] += rng.normal(0.0, 1500.0)
            s, t = place(sequence(p), pred, lats[0], e2, costs[0], hops[0])
            v = value(s, e2, t, wide)
            if v <= val or rng.random() < math.exp((val - v) / (heat * (1 - k / many) + 1)):
                val, end, start, eng, prio = v, t, s, e2, (list(s) if rng.random() < 0.1 else p)
                if v < best[0]:
                    best = (v, s, e2, t)
        val, start, eng, end = best
    return sorted(range(n), key=lambda i: (start[i], i)), eng, start, val


def emit_all(g, T, ops, order, eng):
    queue = {"P": g.tensor, "D": g.vector, "A": g.scalar, "S": g.sync, "G": g}
    pos, cnt = {}, {}
    at = {i: k for k, i in enumerate(order)}
    for i in order:
        if ops[i]["kind"] == "c":
            cnt[eng[i]] = cnt.get(eng[i], 0) + 1
            pos[i] = cnt[eng[i]]
    know = {q: {} for q in queue}
    clock, waits, wanted = {}, {}, set()
    for i in order:
        o = ops[i]
        if o["kind"] == "a":
            clock[i] = {("e", i): 1}
            continue
        k = know[eng[i]]
        need = []
        for j in sorted(o["dep"], key=lambda j: -at[j]):
            p = ops[j]
            if p["kind"] == "s":
                continue
            if p["kind"] == "c":
                if eng[j] == eng[i] and o["kind"] == "c" and not o["dep"][j]:
                    continue
                key, val = eng[j], pos[j]
            else:
                key, val = ("e", j), 1
            if k.get(key, 0) >= val:
                continue
            need.append(j)
            wanted.add(j)
            for a, b in clock[j].items():
                k[a] = max(k.get(a, 0), b)
        waits[i] = need
        c = dict(k)
        if o["kind"] == "c":
            c[eng[i]] = max(c.get(eng[i], 0), pos[i])
        else:
            c[("e", i)] = 1
        clock[i] = c
    sem, tick, nd, ns = {}, {}, 0, 0
    for i in order:
        o = ops[i]
        if o["kind"] == "c" and i in wanted:
            tick[eng[i]] = tick.get(eng[i], 0) + 1
            sem[i] = ("c" + eng[i], tick[eng[i]])
        elif o["kind"] == "d":
            sem[i] = ("dm%d" % nd, 16)
            nd += 1
        elif o["kind"] == "a":
            sem[i] = o["sem"]
    for i in order:
        o = ops[i]
        if o["kind"] == "a":
            continue
        for j in waits[i]:
            queue[eng[i]].wait_ge(T.sem[sem[j][0]], sem[j][1])
        r = o["alts"][eng[i]][0](g)
        if o["kind"] == "s":
            ns += 1
        elif i in sem:
            r.then_inc(T.sem[sem[i][0]], 16 if o["kind"] == "d" else 1)
    g.wait_ge(T.sem.sent, ns * 2 * (N - 1))
    for i in order:
        if ops[i]["kind"] in "da" and i not in wanted:
            g.wait_ge(T.sem[sem[i][0]], sem[i][1])


PLAN = {"rounds": [(14000, 100.0), (12000, 40.0)]}


def rank_program(g, core, T, topo):
    rank = T.rank_of(core)
    if rank is None:
        return
    ops = build(rank, T, topo, GUESS[0])
    depend(ops)
    if "order" not in PLAN:
        versions = [ops] + [build(rank, T, topo, x) for x in GUESS[1:]]
        PLAN["order"], PLAN["eng"], PLAN["start"], PLAN["end"] = improve(versions, PLAN["rounds"])
    emit_all(g, T, ops, PLAN["order"], PLAN["eng"])
